import numpy as np
import ml_dtypes


def mxq(x, axis, fmt="e4m3"):
    dtype, down = {"e4m3": (ml_dtypes.float8_e4m3fn, 7), "e5m2": (ml_dtypes.float8_e5m2, 14)}[fmt]
    v = np.moveaxis(np.asarray(x, np.float32).astype(ml_dtypes.bfloat16).astype(np.float64), axis, -1)
    blocks = v.reshape(v.shape[:-1] + (-1, 32))
    amax = np.abs(blocks).max(-1, keepdims=True)
    byte = np.maximum(np.where(amax > 0, np.frexp(amax)[1] - 1 + 127, 0) - down, 1)
    scale = np.exp2(byte - 127.0)
    codes = (blocks / scale).astype(np.float32).astype(dtype).astype(np.float64)
    return np.moveaxis((codes * scale).reshape(v.shape), -1, axis)


WIDE = False


def mx_kscale(k):
    if not WIDE:
        return np.ones(k)
    levels = np.array([10, -10, 5, -5, 0])
    if k % 512:
        return np.exp2(np.random.permutation(np.resize(levels, k // 32))).repeat(32)
    a = np.empty((k // 512, 16))
    for p in range(k // 512):
        a[p, :8] = np.random.permutation(np.resize(levels, 8))
        for g in range(8):
            far = levels[np.abs(levels - a[p, g]) >= 10]
            a[p, g + 8] = far[np.random.randint(len(far))]
    return np.exp2(a.ravel()).repeat(32)


def f64(x):
    return np.asarray(x).astype(np.float64)


def striped(idx):
    return np.tile(idx.reshape(-1, 16).T, (8, 1)).astype(np.uint16)


def unstriped(offs):
    return offs[:16].T.reshape(-1).astype(np.int64)


E2M1 = np.array([0.0, 0.5, 1.0, 1.5, 2.0, 3.0, 4.0, 6.0, -0.0, -0.5, -1.0, -1.5, -2.0, -3.0, -4.0, -6.0])


def pack_weight(w, fmt):
    k, n = w.shape
    w = f64(np.asarray(w, np.float32).astype(ml_dtypes.bfloat16)).reshape(k // 32, 32, n)
    amax = np.abs(w).max(1)
    if fmt == "e4m3":
        byte = np.frexp(amax)[1] - 1 + 127 - 7
    else:
        mant, ex = np.frexp(amax / 6.0)
        byte = np.where(mant > 0.5, ex, ex - 1) + 127
    byte = np.clip(np.where(amax > 0, byte, 1), 1, 254)
    scaled = (w * np.exp2(127.0 - byte)[:, None, :]).reshape(k, n).astype(np.float32)
    by_word = np.ascontiguousarray(scaled.reshape(k // 512, 128, 4, n).transpose(0, 1, 3, 2))
    if fmt == "e4m3":
        words = by_word.astype(ml_dtypes.float8_e4m3fn).view(np.uint8)
    else:
        c = by_word.astype(ml_dtypes.float4_e2m1fn).view(np.uint8) & 0xF
        words = (c[..., 0::2] | (c[..., 1::2] << 4)).reshape(k // 512, 128, 2 * n)
    return np.ascontiguousarray(words), np.ascontiguousarray(byte.astype(np.uint8).reshape(k // 512, 16, n))


def unpack_weight(words, scales, fmt):
    g, _, n = scales.shape
    words = np.ascontiguousarray(words).reshape(g, 128, n, -1)
    if fmt == "e4m3":
        vals = words.view(ml_dtypes.float8_e4m3fn).astype(np.float64)
    else:
        nib = np.empty((g, 128, n, 4), np.uint8)
        nib[..., 0::2] = words & 0xF
        nib[..., 1::2] = words >> 4
        vals = E2M1[nib]
    vals = vals * np.repeat(np.exp2(scales.astype(np.float64) - 127.0), 8, axis=1)[..., None]
    return vals.transpose(0, 1, 3, 2).reshape(g * 512, n)


def gelu(v):
    return 0.5 * v * (1.0 + np.tanh(np.sqrt(2.0 / np.pi) * (v + 0.044715 * v**3)))


def bf(x):
    return np.asarray(x, np.float32).astype(ml_dtypes.bfloat16)


def planes(Y):
    n, m = Y.shape
    b = f64(bf(Y)).reshape(n // 32, 32, m)
    amax = np.abs(b).max(1)
    byte = np.clip(np.where(amax > 0, np.frexp(amax)[1] - 1 + 127 - 7, 1), 1, 254)
    codes = (b * np.exp2(127.0 - byte)[:, None, :]).reshape(n, m).astype(np.float32).astype(ml_dtypes.float8_e4m3fn).view(np.uint8)
    words = codes.reshape(n // 512, 128, 4, m).transpose(0, 1, 3, 2)
    return np.ascontiguousarray(words), np.ascontiguousarray(byte.astype(np.uint8).reshape(n // 512, 16, m))


K, H, N, T, S, T2, P = 1024, 1024, 512, 4096, 1024, 2048, 1024

def setup_inputs():
    n = np.random.standard_normal
    s = mx_kscale(K)[:, None]
    u = mx_kscale(H)[:, None]
    lev = np.exp(0.8 * n((1, N)))
    tab = pack_weight(n((K, T)) * s, "e4m3")
    w1 = pack_weight(0.8 * n((K, H)) / np.sqrt(K) / s * u.T, "e2m1")
    w4 = pack_weight(n((H, N)) / np.sqrt(H) / u * lev, "e4m3")
    return {
        "tab_words": tab[0], "tab_scales": tab[1],
        "offs": striped(np.random.permutation(T)[:S]),
        "w1_words": w1[0], "w1_scales": w1[1],
        "wgs": np.exp(0.3 * n((128, S))).astype(np.float32),
        "offs2": striped(np.random.permutation(T2)[:S]),
        "offs3": striped(np.random.permutation(T2)[:P]),
        "noise": (0.7 * n((H, P)) * u ** 2).astype(np.float32),
        "bend": (np.random.uniform(0.4, 1.2, H) / u[:, 0] ** 2).astype(np.float32),
        "gain": (np.random.uniform(0.7, 2.0, H) * u[:, 0]).astype(np.float32),
        "w3": (0.8 * n((H, N)) / np.sqrt(H) / u ** 2 * lev).astype(np.float32),
        "w4_words": w4[0], "w4_scales": w4[1],
    }

def reference(tab_words, tab_scales, offs, w1_words, w1_scales, wgs, offs2, offs3,
              noise, bend, gain, w3, w4_words, w4_scales):
    v = unpack_weight(tab_words, tab_scales, "e4m3")[:, unstriped(offs)]
    w1 = unpack_weight(w1_words, w1_scales, "e2m1")
    w4 = unpack_weight(w4_words, w4_scales, "e4m3")
    h = np.square(w1.T @ v)
    page = np.zeros((H, T2))
    page[:, unstriped(offs2)] = np.tile(f64(wgs), (H // 128, 1)) * h
    x = page[:, unstriped(offs3)]
    z = x + f64(noise)
    d = np.tanh(z * f64(bend)[:, None]) * f64(gain)[:, None]
    zq = mxq(z, 0, "e4m3")
    dq = mxq(d, 0, "e4m3")
    y = mxq(f64(w3), 0, "e4m3").T @ zq + w4.T @ dq
    words, scales = planes(y)
    return y, words, scales

@@ -1,0 +1,304 @@
+from contextlib import ExitStack
+
+import concourse.mybir as mybir
+
+F32 = mybir.dt.float32
+BF16 = mybir.dt.bfloat16
+I32 = mybir.dt.int32
+U32 = mybir.dt.uint32
+U16 = mybir.dt.uint16
+U8 = mybir.dt.uint8
+FP8X4 = mybir.dt.float8_e4m3fn_x4
+FP4X4 = mybir.dt.float4_e2m1fn_x4
+ACT = mybir.ActivationFunctionType
+ALU = mybir.AluOpType
+
+K, H, N, T, S, T2, M = 1024, 1024, 512, 4096, 1024, 2048, 1024
+FLOPS = 2 * K * H * S + 2 * 2 * H * N * M
+
+P = 128
+PACK = 4
+PASSES = 2
+SLICES = PASSES * PACK
+HALF = 512
+BANK_M = 128
+TAIL_M = 256
+HW_MOVES = 6
+
+
+def tile_list_packet_loss_concealer_kernel(
+    tc, tab_words, tab_scales, offs, w1_words, w1_scales, wgs, offs2, offs3,
+    noise, bend, gain, w3, w4_words, w4_scales, out_0, out_1, out_2,
+):
+    nc = tc.nc
+    with ExitStack() as ctx:
+        lists = ctx.enter_context(tc.tile_pool(name="lists", bufs=1))
+        sb = ctx.enter_context(tc.tile_pool(name="sb", bufs=1))
+        psum = ctx.enter_context(tc.psum_pool(name="psum", bufs=1))
+
+        def alloc(shape, dtype, name, tag=None, bufs=1):
+            return sb.tile(shape, dtype, name=name, tag=tag or name, bufs=bufs, align_bytes=64)
+
+        idx = lists.tile([P, S // 16], U16, name="idx")
+        idx2 = lists.tile([P, S // 16], U16, name="idx2")
+        idx3 = lists.tile([P, M // 16], U16, name="idx3")
+        nc.sync.dma_start(idx[:], offs)
+        nc.sync.dma_start(idx2[:], offs2)
+        nc.sync.dma_start(idx3[:], offs3)
+
+        tab_sc = alloc([P, T], U8, "tab_sc", tag="sc_then_wgs")
+        nc.sync.dma_start(tab_sc[0:32, :].bitcast(I32), tab_scales.rearrange("a q t -> (a q) t").bitcast(I32))
+        nc.vector.memset(tab_sc[32:64, :].bitcast(I32), 0)
+        nc.vector.memset(tab_sc[64:128, :].bitcast(I32), 0)
+        w1_raw = alloc([P, PASSES, 2 * H], U8, "w1_raw")
+        nc.sync.dma_start(w1_raw[:].bitcast(I32), w1_words.rearrange("a p c -> p a c").bitcast(I32))
+        tab_w = []
+        for a in range(PASSES):
+            t_w = alloc([P, T], I32, "tab_w%d" % a, tag="big%d" % a)
+            nc.sync.dma_start(t_w[:], tab_words[a].rearrange("p t i -> p (t i)").bitcast(I32))
+            tab_w.append(t_w)
+        w1_sc_raw = alloc([P, PASSES, H], U8, "w1_sc_raw")
+        nc.gpsimd.memset(w1_sc_raw[:].rearrange("p a c -> p (a c)").bitcast(I32), 0)
+        for q in range(4):
+            nc.gpsimd.dma_start(
+                w1_sc_raw[32 * q : 32 * q + 4, :, :].bitcast(I32),
+                w1_scales[:, 4 * q : 4 * q + 4, :].rearrange("a r c -> r a c").bitcast(I32),
+            )
+        v_sc = alloc([P, PASSES, S], U8, "v_sc", tag="vsc_then_w3")
+        nc.gpsimd.memset(v_sc[:].rearrange("p a c -> p (a c)").bitcast(I32), 0)
+
+        picked_sc = alloc([P, S], U8, "picked_sc")
+        nc.vector.tensor_copy(picked_sc[:], tab_sc[:].indirect(idx[:]))
+        for n_move in range(PASSES * 4):
+            a, q = divmod(n_move, 4)
+            queue = nc.scalar if n_move < HW_MOVES else nc.gpsimd
+            row = 16 * a + 4 * q
+            queue.dma_start(v_sc[32 * q : 32 * q + 4, a, :].bitcast(I32), picked_sc[row : row + 4, :].bitcast(I32))
+
+        wgs_rows = wgs.rearrange("(i t) j -> i t j", t=PACK)
+        wgs_first = alloc([P, S], F32, "wgs_first", tag="sc_then_wgs")
+        for q in range(4):
+            nc.sync.dma_start(wgs_first[32 * q : 32 * q + 32, :], wgs_rows[:, 0, :])
+
+        w1_w, w1_sc = [], []
+        for b in range(PASSES):
+            dealt = alloc([P, PASSES, 2 * HALF], U8, "w1_w%d" % b, tag="w1w%d" % b)
+            nc.vector.tensor_copy(
+                dealt[:].bitcast(U16).rearrange("p a (t m) -> p a t m", t=PACK),
+                w1_raw[:].bitcast(U16)[:, :, b * HALF : (b + 1) * HALF].rearrange("p a (m t) -> p a t m", t=PACK),
+            )
+            w1_w.append(dealt)
+        for b in range(PASSES):
+            dealt = alloc([P, PASSES, HALF], U8, "w1_sc%d" % b, tag=("z_sc0", "z_w0")[b])
+            nc.vector.tensor_copy(
+                dealt[:].rearrange("p a (t m) -> p a t m", t=PACK),
+                w1_sc_raw[:, :, b * HALF : (b + 1) * HALF].rearrange("p a (m t) -> p a t m", t=PACK),
+            )
+            w1_sc.append(dealt)
+
+        v_w = alloc([P, PASSES, S], U32, "v_w", tag="vw_then_noise")
+        nc.vector.tensor_copy(v_w[:, 0, :], tab_w[0][:].bitcast(U32).indirect(idx[:]))
+        for half in range(2):
+            nc.vector.tensor_copy(
+                v_w[:, 1, half * HALF : (half + 1) * HALF],
+                tab_w[1][:].bitcast(U32).indirect(idx[:, half * 32 : (half + 1) * 32]),
+            )
+
+        pages = [alloc([P, T2], F32, "page%d" % i) for i in range(2)]
+        for page in pages:
+            nc.vector.memset(page[:], 0.0)
+
+        wgs_rest = alloc([P, PACK - 1, S], F32, "wgs_rest", tag="big0")
+        for q in range(4):
+            nc.sync.dma_start(wgs_rest[32 * q : 32 * q + 32, :, :], wgs_rows[:, 1:PACK, :])
+        noise_rows = noise.rearrange("(b p t) m -> b p t m", b=PASSES, t=PACK)
+        noise_sb = [alloc([P, PACK, M], F32, "noise0", tag="big1"), None]
+        for u in range(2):
+            nc.sync.dma_start(noise_sb[0][:, 2 * u : 2 * u + 2, :], noise_rows[0][:, 2 * u : 2 * u + 2, :])
+        bend_sb = alloc([P, PASSES, PACK], F32, "bend_sb")
+        gain_sb = alloc([P, PASSES, PACK], F32, "gain_sb")
+        nc.gpsimd.dma_start(bend_sb[:], bend.rearrange("(b p t) -> p b t", b=PASSES, t=PACK))
+        nc.gpsimd.dma_start(gain_sb[:], gain.rearrange("(b p t) -> p b t", b=PASSES, t=PACK))
+
+        h_sb = {}
+
+        def project(s):
+            b, t = divmod(s, PACK)
+            h_sb[s] = alloc([P, S], F32, "h%d" % s, tag="h_then_y", bufs=4)
+            for half in range(2):
+                cols = slice(half * HALF, (half + 1) * HALF)
+                bank = psum.tile([P, HALF], F32, name="hbank%d_%d" % (s, half), tag="bank%d" % ((2 * s + half) % 8))
+                for a in range(PASSES):
+                    nc.tensor.matmul_mx(
+                        out=bank[:],
+                        lhsT=w1_w[b][:, a, 2 * P * t : 2 * P * (t + 1)].bitcast(FP4X4),
+                        lhsT_scale=w1_sc[b][:, a, P * t : P * (t + 1)],
+                        rhs=v_w[:, a, cols].bitcast(FP8X4),
+                        rhs_scale=v_sc[:, a, cols],
+                        start=(a == 0),
+                        stop=(a == PASSES - 1),
+                    )
+                nc.scalar.activation(h_sb[s][:, cols], bank[:], ACT.Square)
+
+        def scatter(s):
+            t = s % PACK
+            weight = wgs_first[:] if t == 0 else wgs_rest[:, t - 1, :]
+            page = pages[page_of(s)]
+            pieces = 2 if s == 0 else 1
+            width = S // pieces
+            for i in range(pieces):
+                cols = slice(i * width, (i + 1) * width)
+                nc.vector.tensor_tensor(
+                    page[:].indirect(idx2[:, i * width // 16 : (i + 1) * width // 16]),
+                    h_sb[s][:, cols], weight[:, cols], ALU.mult,
+                )
+
+        def page_of(s):
+            return s % 2 if s < SLICES - 1 else (s - 1) % 2
+
+        z_pair = {}
+        z_bf, d_bf = {}, {}
+
+        def gather(s, cols):
+            b, t = divmod(s, PACK)
+            nc.vector.tensor_tensor(
+                z_pair[s // 2][:, s % 2, cols],
+                pages[page_of(s)][:].indirect(idx3[:, cols.start // 16 : cols.stop // 16]),
+                noise_sb[b][:, t, cols], ALU.add,
+            )
+
+        def bend_plane(s, cols):
+            b, t = divmod(s, PACK)
+            width = cols.stop - cols.start
+            tanh = alloc([P, width], F32, "tanh%d_%d" % (s, cols.start), tag="tanh", bufs=2)
+            nc.scalar.activation(tanh[:], z_pair[s // 2][:, s % 2, cols], ACT.Tanh, scale=bend_sb[:, b, t : t + 1])
+            nc.scalar.activation(d_bf[b][:, cols, t], tanh[:], ACT.Copy, scale=gain_sb[:, b, t : t + 1])
+
+        def round_pair(pair, cols, copy):
+            b, u = divmod(pair, 2)
+            copy(z_bf[b][:, cols, 2 * u : 2 * u + 2], z_pair[pair][:, :, cols].rearrange("p e m -> p m e"))
+
+        codes = {}
+
+        def quantise(name, b, source, cols):
+            words, scales = codes[name, b]
+            nc.vector.quantize_mx(
+                out=words[:, cols].bitcast(FP8X4),
+                scales=scales[:, cols],
+                in_=source[:, cols, :].rearrange("p m t -> p (m t)"),
+            )
+
+        def second_weights():
+            w3_rows = w3.rearrange("(b p j) n -> b p j n", b=PASSES, j=PACK)
+            for b in range(PASSES):
+                raw = alloc([P, PACK, N], F32, "w3_raw%d" % b, tag=("vsc_then_w3", "w1w1")[b])
+                nc.sync.dma_start(raw[:], w3_rows[b])
+                grouped = alloc([P, N, PACK], BF16, "w3_bf%d" % b, tag=("d_sc0", "d_w0")[b])
+                nc.scalar.copy(
+                    grouped[:].rearrange("p (t m) j -> p t m j", t=PACK),
+                    raw[:].rearrange("p j (m t) -> p t m j", t=PACK),
+                )
+                codes["w3", b] = (alloc([P, N], U32, "w3_w%d" % b), alloc([P, N], U8, "w3_sc%d" % b))
+                quantise("w3", b, grouped, slice(0, N))
+            w4_raw = alloc([P, PASSES, N], I32, "w4_raw", tag="z_w0")
+            nc.sync.dma_start(w4_raw[:], w4_words.rearrange("a p c i -> p a (c i)").bitcast(I32))
+            w4_sc_raw = alloc([P, PASSES, N], U8, "w4_sc_raw", tag="z_sc0")
+            nc.gpsimd.memset(w4_sc_raw[:].rearrange("p a c -> p (a c)").bitcast(I32), 0)
+            for q in range(4):
+                nc.gpsimd.dma_start(
+                    w4_sc_raw[32 * q : 32 * q + 4, :, :].bitcast(I32),
+                    w4_scales[:, 4 * q : 4 * q + 4, :].rearrange("a r c -> r a c").bitcast(I32),
+                )
+            w4_w = alloc([P, PASSES, N], I32, "w4_w")
+            w4_sc = alloc([P, PASSES, N], U8, "w4_sc")
+            for dealt, raw in ((w4_w, w4_raw), (w4_sc, w4_sc_raw)):
+                nc.vector.tensor_copy(
+                    dealt[:].rearrange("p a (t m) -> p a t m", t=PACK),
+                    raw[:].rearrange("p a (m t) -> p a t m", t=PACK),
+                )
+            for b in range(PASSES):
+                codes["w4", b] = (w4_w[:, b, :], w4_sc[:, b, :])
+
+        y_banks = {}
+
+        def multiply(b, c):
+            cols = slice(c * BANK_M, (c + 1) * BANK_M)
+            if b == 0:
+                y_banks[c] = psum.tile([P, PACK, BANK_M], F32, name="ybank%d" % c, tag="bank%d" % c)
+            for i, (weight, moving) in enumerate((("w3", "z"), ("w4", "d"))):
+                for t in range(PACK):
+                    n_cols = slice(t * P, (t + 1) * P)
+                    nc.tensor.matmul_mx(
+                        out=y_banks[c][:, t, :],
+                        lhsT=codes[weight, b][0][:, n_cols].bitcast(FP8X4),
+                        lhsT_scale=codes[weight, b][1][:, n_cols],
+                        rhs=codes[moving, b][0][:, cols].bitcast(FP8X4),
+                        rhs_scale=codes[moving, b][1][:, cols],
+                        start=(b == 0 and i == 0 and t == 0),
+                        stop=(b == PASSES - 1 and i == 1 and t == PACK - 1),
+                    )
+
+        def open_slice(s):
+            b, t = divmod(s, PACK)
+            if s % 2 == 0:
+                z_pair[s // 2] = alloc([P, 2, M], F32, "z_pair%d" % (s // 2), tag=("z_pair0", "z_pair1", "z_pair0", "d_bf0")[s // 2])
+            if t == 0:
+                z_bf[b] = alloc([P, M, PACK], BF16, "z_bf%d" % b)
+                d_bf[b] = alloc([P, M, PACK], BF16, "d_bf%d" % b)
+                for name in ("z", "d"):
+                    codes[name, b] = (alloc([P, M], U32, "%s_w%d" % (name, b)), alloc([P, M], U8, "%s_sc%d" % (name, b)))
+
+        everything = slice(0, M)
+        for s in range(4):
+            project(s)
+        scatter(0)
+        for s in range(SLICES - 1):
+            if s + 4 < SLICES:
+                project(s + 4)
+            if s + 1 < SLICES - 1:
+                scatter(s + 1)
+            if s == 3:
+                noise_sb[1] = alloc([P, PACK, M], F32, "noise1", tag="vw_then_noise")
+                nc.sync.dma_start(noise_sb[1][:], noise_rows[1])
+                second_weights()
+            open_slice(s)
+            gather(s, everything)
+            bend_plane(s, everything)
+            if s % 2 == 1:
+                round_pair(s // 2, everything, nc.scalar.copy)
+            if s == PACK - 1:
+                quantise("z", 0, z_bf[0], everything)
+                quantise("d", 0, d_bf[0], everything)
+                for c in range(M // BANK_M):
+                    multiply(0, c)
+
+        last = SLICES - 1
+        scatter(last)
+        chunks = [slice(c0, c0 + TAIL_M) for c0 in range(0, M, TAIL_M)]
+        y_rows = out_0.rearrange("(p t) m -> p t m", t=PACK)
+        y_words = alloc([P, M], I32, "y_words")
+        y_scales = alloc([P, M], U8, "y_scales")
+        codes["y", 0] = (y_words, y_scales)
+        y_bf = alloc([P, M, PACK], BF16, "y_bf", tag="big1")
+        out_words = out_1[0].rearrange("p m t -> p (m t)").bitcast(I32)
+        for cols in chunks:
+            gather(last, cols)
+            bend_plane(last, cols)
+        y_sb = {}
+        for cols in chunks:
+            round_pair(last // 2, cols, nc.vector.tensor_copy)
+            quantise("z", 1, z_bf[1], cols)
+            quantise("d", 1, d_bf[1], cols)
+            y_sb[cols.start] = alloc([P, PACK, TAIL_M], F32, "y%d" % cols.start, tag="h_then_y", bufs=4)
+            for i, c in enumerate(range(cols.start // BANK_M, cols.stop // BANK_M)):
+                multiply(1, c)
+                nc.scalar.copy(y_sb[cols.start][:, :, i * BANK_M : (i + 1) * BANK_M], y_banks[c][:])
+            nc.sync.dma_start(y_rows[:, :, cols], y_sb[cols.start][:])
+        for cols in chunks:
+            copy = nc.scalar.copy if cols.start == 0 else nc.vector.tensor_copy
+            copy(y_bf[:, cols, :], y_sb[cols.start][:].rearrange("p t m -> p m t"))
+            quantise("y", 0, y_bf, cols)
+            nc.sync.dma_start(out_words[:, cols], y_words[:, cols])
+        for q in range(4):
+            queue = nc.sync if q % 2 == 0 else nc.scalar
+            queue.dma_start(out_2[0][4 * q : 4 * q + 4, :].bitcast(I32), y_scales[32 * q : 32 * q + 4, :].bitcast(I32))

@@ -46,41 +46,43 @@ def tile_list_packet_loss_concealer_kernel(
         nc.sync.dma_start(idx2[:], offs2)
         nc.sync.dma_start(idx3[:], offs3)
 
-        tab_sc = alloc([P, T], U8, "tab_sc", tag="sc_then_wgs")
+        tab_sc = alloc([P, T], U8, "tab_sc")
+        w1_sc_raw = alloc([P, H], U8, "w1_sc_raw", tag="page0")
         nc.sync.dma_start(tab_sc[0:32, :].bitcast(I32), tab_scales.rearrange("a q t -> (a q) t").bitcast(I32))
-        nc.vector.memset(tab_sc[32:64, :].bitcast(I32), 0)
-        nc.vector.memset(tab_sc[64:128, :].bitcast(I32), 0)
-        w1_raw = alloc([P, PASSES, 2 * H], U8, "w1_raw")
+        nc.sync.dma_start(w1_sc_raw[0:32, :].bitcast(I32), w1_scales.rearrange("a q c -> (a q) c").bitcast(I32))
+        for rows in (tab_sc, w1_sc_raw):
+            nc.vector.memset(rows[32:64, :].bitcast(I32), 0)
+            nc.vector.memset(rows[64:128, :].bitcast(I32), 0)
+        w1_raw = alloc([P, PASSES, 2 * H], U8, "w1_raw", tag="page1")
         nc.sync.dma_start(w1_raw[:].bitcast(I32), w1_words.rearrange("a p c -> p a c").bitcast(I32))
         tab_w = []
         for a in range(PASSES):
             t_w = alloc([P, T], I32, "tab_w%d" % a, tag="big%d" % a)
             nc.sync.dma_start(t_w[:], tab_words[a].rearrange("p t i -> p (t i)").bitcast(I32))
             tab_w.append(t_w)
-        w1_sc_raw = alloc([P, PASSES, H], U8, "w1_sc_raw")
-        nc.gpsimd.memset(w1_sc_raw[:].rearrange("p a c -> p (a c)").bitcast(I32), 0)
-        for q in range(4):
-            nc.gpsimd.dma_start(
-                w1_sc_raw[32 * q : 32 * q + 4, :, :].bitcast(I32),
-                w1_scales[:, 4 * q : 4 * q + 4, :].rearrange("a r c -> r a c").bitcast(I32),
-            )
-        v_sc = alloc([P, PASSES, S], U8, "v_sc", tag="vsc_then_w3")
-        nc.gpsimd.memset(v_sc[:].rearrange("p a c -> p (a c)").bitcast(I32), 0)
+        planes = alloc([P, PASSES, S + H], U8, "planes")
+        nc.vector.memset(planes[:].rearrange("p a c -> p (a c)").bitcast(I32), 0)
 
         picked_sc = alloc([P, S], U8, "picked_sc")
         nc.vector.tensor_copy(picked_sc[:], tab_sc[:].indirect(idx[:]))
+        staged = alloc([P, S + H], U8, "staged")
+        nc.vector.tensor_copy(
+            staged[:, S : S + H].rearrange("p (b t m) -> p b t m", b=PASSES, t=PACK),
+            w1_sc_raw[:].rearrange("p (b m t) -> p b t m", b=PASSES, t=PACK),
+        )
+        nc.vector.tensor_copy(staged[:, 0:S].bitcast(I32), picked_sc[:].bitcast(I32))
         for n_move in range(PASSES * 4):
             a, q = divmod(n_move, 4)
-            queue = nc.scalar if n_move < HW_MOVES else nc.gpsimd
+            queue = nc.sync if n_move < HW_MOVES else nc.gpsimd
             row = 16 * a + 4 * q
-            queue.dma_start(v_sc[32 * q : 32 * q + 4, a, :].bitcast(I32), picked_sc[row : row + 4, :].bitcast(I32))
+            queue.dma_start(planes[32 * q : 32 * q + 4, a, :].bitcast(I32), staged[row : row + 4, :].bitcast(I32))
 
         wgs_rows = wgs.rearrange("(i t) j -> i t j", t=PACK)
-        wgs_first = alloc([P, S], F32, "wgs_first", tag="sc_then_wgs")
+        wgs_first = alloc([P, S], F32, "wgs_first", tag="picked_sc")
         for q in range(4):
             nc.sync.dma_start(wgs_first[32 * q : 32 * q + 32, :], wgs_rows[:, 0, :])
 
-        w1_w, w1_sc = [], []
+        w1_w = []
         for b in range(PASSES):
             dealt = alloc([P, PASSES, 2 * HALF], U8, "w1_w%d" % b, tag="w1w%d" % b)
             nc.vector.tensor_copy(
@@ -88,21 +90,14 @@ def tile_list_packet_loss_concealer_kernel(
                 w1_raw[:].bitcast(U16)[:, :, b * HALF : (b + 1) * HALF].rearrange("p a (m t) -> p a t m", t=PACK),
             )
             w1_w.append(dealt)
-        for b in range(PASSES):
-            dealt = alloc([P, PASSES, HALF], U8, "w1_sc%d" % b, tag=("z_sc0", "z_w0")[b])
-            nc.vector.tensor_copy(
-                dealt[:].rearrange("p a (t m) -> p a t m", t=PACK),
-                w1_sc_raw[:, :, b * HALF : (b + 1) * HALF].rearrange("p a (m t) -> p a t m", t=PACK),
-            )
-            w1_sc.append(dealt)
 
-        v_w = alloc([P, PASSES, S], U32, "v_w", tag="vw_then_noise")
-        nc.vector.tensor_copy(v_w[:, 0, :], tab_w[0][:].bitcast(U32).indirect(idx[:]))
+        v_first = alloc([P, S], U32, "v_first", tag="vw_then_noise")
+        nc.vector.tensor_copy(v_first[:], tab_w[0][:].bitcast(U32).indirect(idx[:]))
+        v_w = {(0, half): v_first[:, half * HALF : (half + 1) * HALF] for half in range(2)}
         for half in range(2):
-            nc.vector.tensor_copy(
-                v_w[:, 1, half * HALF : (half + 1) * HALF],
-                tab_w[1][:].bitcast(U32).indirect(idx[:, half * 32 : (half + 1) * 32]),
-            )
+            picked = alloc([P, HALF], U32, "v_second%d" % half, tag=("vsc_then_w3", "v_then_w4")[half])
+            nc.vector.tensor_copy(picked[:], tab_w[1][:].bitcast(U32).indirect(idx[:, half * 32 : (half + 1) * 32]))
+            v_w[1, half] = picked[:]
 
         pages = [alloc([P, T2], F32, "page%d" % i) for i in range(2)]
         for page in pages:
@@ -115,16 +110,12 @@ def tile_list_packet_loss_concealer_kernel(
         noise_sb = [alloc([P, PACK, M], F32, "noise0", tag="big1"), None]
         for u in range(2):
             nc.sync.dma_start(noise_sb[0][:, 2 * u : 2 * u + 2, :], noise_rows[0][:, 2 * u : 2 * u + 2, :])
-        bend_sb = alloc([P, PASSES, PACK], F32, "bend_sb")
-        gain_sb = alloc([P, PASSES, PACK], F32, "gain_sb")
-        nc.gpsimd.dma_start(bend_sb[:], bend.rearrange("(b p t) -> p b t", b=PASSES, t=PACK))
-        nc.gpsimd.dma_start(gain_sb[:], gain.rearrange("(b p t) -> p b t", b=PASSES, t=PACK))
 
         h_sb = {}
 
         def project(s):
             b, t = divmod(s, PACK)
-            h_sb[s] = alloc([P, S], F32, "h%d" % s, tag="h_then_y", bufs=4)
+            h_sb[s] = alloc([P, S], F32, "h%d" % s)
             for half in range(2):
                 cols = slice(half * HALF, (half + 1) * HALF)
                 bank = psum.tile([P, HALF], F32, name="hbank%d_%d" % (s, half), tag="bank%d" % ((2 * s + half) % 8))
@@ -132,9 +123,9 @@ def tile_list_packet_loss_concealer_kernel(
                     nc.tensor.matmul_mx(
                         out=bank[:],
                         lhsT=w1_w[b][:, a, 2 * P * t : 2 * P * (t + 1)].bitcast(FP4X4),
-                        lhsT_scale=w1_sc[b][:, a, P * t : P * (t + 1)],
-                        rhs=v_w[:, a, cols].bitcast(FP8X4),
-                        rhs_scale=v_sc[:, a, cols],
+                        lhsT_scale=planes[:, a, S + P * s : S + P * (s + 1)],
+                        rhs=v_w[a, half].bitcast(FP8X4),
+                        rhs_scale=planes[:, a, cols],
                         start=(a == 0),
                         stop=(a == PASSES - 1),
                     )
@@ -170,7 +161,7 @@ def tile_list_packet_loss_concealer_kernel(
         def bend_plane(s, cols):
             b, t = divmod(s, PACK)
             width = cols.stop - cols.start
-            tanh = alloc([P, width], F32, "tanh%d_%d" % (s, cols.start), tag="tanh", bufs=2)
+            tanh = alloc([P, width], F32, "tanh%d_%d" % (s, cols.start), tag=("vsc_then_w3", "w1w1")[(s + cols.start // TAIL_M) % 2])
             nc.scalar.activation(tanh[:], z_pair[s // 2][:, s % 2, cols], ACT.Tanh, scale=bend_sb[:, b, t : t + 1])
             nc.scalar.activation(d_bf[b][:, cols, t], tanh[:], ACT.Copy, scale=gain_sb[:, b, t : t + 1])
 
@@ -193,74 +184,84 @@ def tile_list_packet_loss_concealer_kernel(
             for b in range(PASSES):
                 raw = alloc([P, PACK, N], F32, "w3_raw%d" % b, tag=("vsc_then_w3", "w1w1")[b])
                 nc.sync.dma_start(raw[:], w3_rows[b])
-                grouped = alloc([P, N, PACK], BF16, "w3_bf%d" % b, tag=("d_sc0", "d_w0")[b])
+                grouped = alloc([P, N, PACK], BF16, "w3_bf%d" % b, tag="w3_bf%d" % b)
                 nc.scalar.copy(
                     grouped[:].rearrange("p (t m) j -> p t m j", t=PACK),
                     raw[:].rearrange("p j (m t) -> p t m j", t=PACK),
                 )
                 codes["w3", b] = (alloc([P, N], U32, "w3_w%d" % b), alloc([P, N], U8, "w3_sc%d" % b))
                 quantise("w3", b, grouped, slice(0, N))
-            w4_raw = alloc([P, PASSES, N], I32, "w4_raw", tag="z_w0")
+            w4_raw = alloc([P, PASSES, N], I32, "w4_raw", tag="v_then_w4")
             nc.sync.dma_start(w4_raw[:], w4_words.rearrange("a p c i -> p a (c i)").bitcast(I32))
-            w4_sc_raw = alloc([P, PASSES, N], U8, "w4_sc_raw", tag="z_sc0")
-            nc.gpsimd.memset(w4_sc_raw[:].rearrange("p a c -> p (a c)").bitcast(I32), 0)
+            w4_sc_raw = planes[:, :, 0:N]
             for q in range(4):
-                nc.gpsimd.dma_start(
-                    w4_sc_raw[32 * q : 32 * q + 4, :, :].bitcast(I32),
+                nc.sync.dma_start(
+                    planes[32 * q : 32 * q + 4, :, 0:N].bitcast(I32),
                     w4_scales[:, 4 * q : 4 * q + 4, :].rearrange("a r c -> r a c").bitcast(I32),
                 )
-            w4_w = alloc([P, PASSES, N], I32, "w4_w")
-            w4_sc = alloc([P, PASSES, N], U8, "w4_sc")
+            return w4_raw[:], w4_sc_raw
+
+        def deal_w4(w4_raw, w4_sc_raw):
+            w4_w = alloc([P, PASSES, N], I32, "w4_w", tag="h4")
+            w4_sc = alloc([P, PASSES, N], U8, "w4_sc", tag="h5")
             for dealt, raw in ((w4_w, w4_raw), (w4_sc, w4_sc_raw)):
                 nc.vector.tensor_copy(
                     dealt[:].rearrange("p a (t m) -> p a t m", t=PACK),
-                    raw[:].rearrange("p a (m t) -> p a t m", t=PACK),
+                    raw.rearrange("p a (m t) -> p a t m", t=PACK),
                 )
             for b in range(PASSES):
                 codes["w4", b] = (w4_w[:, b, :], w4_sc[:, b, :])
 
         y_banks = {}
 
-        def multiply(b, c):
+        def multiply(weight, moving, b, c):
             cols = slice(c * BANK_M, (c + 1) * BANK_M)
-            if b == 0:
+            opens = b == 0 and moving == "z"
+            closes = b == PASSES - 1 and moving == "d"
+            if opens:
                 y_banks[c] = psum.tile([P, PACK, BANK_M], F32, name="ybank%d" % c, tag="bank%d" % c)
-            for i, (weight, moving) in enumerate((("w3", "z"), ("w4", "d"))):
-                for t in range(PACK):
-                    n_cols = slice(t * P, (t + 1) * P)
-                    nc.tensor.matmul_mx(
-                        out=y_banks[c][:, t, :],
-                        lhsT=codes[weight, b][0][:, n_cols].bitcast(FP8X4),
-                        lhsT_scale=codes[weight, b][1][:, n_cols],
-                        rhs=codes[moving, b][0][:, cols].bitcast(FP8X4),
-                        rhs_scale=codes[moving, b][1][:, cols],
-                        start=(b == 0 and i == 0 and t == 0),
-                        stop=(b == PASSES - 1 and i == 1 and t == PACK - 1),
-                    )
+            for t in range(PACK):
+                n_cols = slice(t * P, (t + 1) * P)
+                nc.tensor.matmul_mx(
+                    out=y_banks[c][:, t, :],
+                    lhsT=codes[weight, b][0][:, n_cols].bitcast(FP8X4),
+                    lhsT_scale=codes[weight, b][1][:, n_cols],
+                    rhs=codes[moving, b][0][:, cols].bitcast(FP8X4),
+                    rhs_scale=codes[moving, b][1][:, cols],
+                    start=(opens and t == 0),
+                    stop=(closes and t == PACK - 1),
+                )
+
+        def banks_of(cols):
+            return range(cols.start // BANK_M, cols.stop // BANK_M)
 
         def open_slice(s):
             b, t = divmod(s, PACK)
             if s % 2 == 0:
-                z_pair[s // 2] = alloc([P, 2, M], F32, "z_pair%d" % (s // 2), tag=("z_pair0", "z_pair1", "z_pair0", "d_bf0")[s // 2])
+                z_pair[s // 2] = alloc([P, 2, M], F32, "z_pair%d" % (s // 2), tag=("z_pair0", "z_pair1", "z_pair0", "z_bf0")[s // 2])
             if t == 0:
                 z_bf[b] = alloc([P, M, PACK], BF16, "z_bf%d" % b)
                 d_bf[b] = alloc([P, M, PACK], BF16, "d_bf%d" % b)
                 for name in ("z", "d"):
-                    codes[name, b] = (alloc([P, M], U32, "%s_w%d" % (name, b)), alloc([P, M], U8, "%s_sc%d" % (name, b)))
+                    if (name, b) != ("d", 0):
+                        codes[name, b] = (alloc([P, M], U32, "%s_w%d" % (name, b)), alloc([P, M], U8, "%s_sc%d" % (name, b)))
 
         everything = slice(0, M)
-        for s in range(4):
+        for s in range(SLICES):
             project(s)
+        factors = alloc([P, 2, PASSES, PACK], F32, "factors", tag="w1w0")
+        bend_sb, gain_sb = factors[:, 0], factors[:, 1]
+        nc.sync.dma_start(bend_sb, bend.rearrange("(b p t) -> p b t", b=PASSES, t=PACK))
+        nc.sync.dma_start(gain_sb, gain.rearrange("(b p t) -> p b t", b=PASSES, t=PACK))
+        w4_loaded = second_weights()
+        noise_sb[1] = alloc([P, PACK, M], F32, "noise1", tag="vw_then_noise")
+        nc.sync.dma_start(noise_sb[1][:], noise_rows[1])
         scatter(0)
         for s in range(SLICES - 1):
-            if s + 4 < SLICES:
-                project(s + 4)
             if s + 1 < SLICES - 1:
                 scatter(s + 1)
-            if s == 3:
-                noise_sb[1] = alloc([P, PACK, M], F32, "noise1", tag="vw_then_noise")
-                nc.sync.dma_start(noise_sb[1][:], noise_rows[1])
-                second_weights()
+            if s == 4:
+                deal_w4(*w4_loaded)
             open_slice(s)
             gather(s, everything)
             bend_plane(s, everything)
@@ -268,9 +269,8 @@ def tile_list_packet_loss_concealer_kernel(
                 round_pair(s // 2, everything, nc.scalar.copy)
             if s == PACK - 1:
                 quantise("z", 0, z_bf[0], everything)
-                quantise("d", 0, d_bf[0], everything)
-                for c in range(M // BANK_M):
-                    multiply(0, c)
+                for c in banks_of(everything):
+                    multiply("w3", "z", 0, c)
 
         last = SLICES - 1
         scatter(last)
@@ -281,24 +281,42 @@ def tile_list_packet_loss_concealer_kernel(
         codes["y", 0] = (y_words, y_scales)
         y_bf = alloc([P, M, PACK], BF16, "y_bf", tag="big1")
         out_words = out_1[0].rearrange("p m t -> p (m t)").bitcast(I32)
+        codes["d", 0] = (alloc([P, M], U32, "d_w0", tag="h%d" % last), alloc([P, M], U8, "d_sc0"))
         for cols in chunks:
             gather(last, cols)
             bend_plane(last, cols)
+            quantise("d", 0, d_bf[0], cols)
+            for c in banks_of(cols):
+                multiply("w4", "d", 0, c)
+        for cols in chunks[2:]:
+            round_pair(last // 2, cols, nc.scalar.copy)
         y_sb = {}
-        for cols in chunks:
-            round_pair(last // 2, cols, nc.vector.tensor_copy)
+        for n_chunk, cols in enumerate(chunks):
+            if n_chunk < 2:
+                round_pair(last // 2, cols, nc.vector.tensor_copy)
             quantise("z", 1, z_bf[1], cols)
             quantise("d", 1, d_bf[1], cols)
-            y_sb[cols.start] = alloc([P, PACK, TAIL_M], F32, "y%d" % cols.start, tag="h_then_y", bufs=4)
-            for i, c in enumerate(range(cols.start // BANK_M, cols.stop // BANK_M)):
-                multiply(1, c)
+            y_sb[cols.start] = alloc([P, PACK, TAIL_M], F32, "y%d" % cols.start, tag="h%d" % n_chunk)
+            for i, c in enumerate(banks_of(cols)):
+                multiply("w3", "z", 1, c)
+                multiply("w4", "d", 1, c)
                 nc.scalar.copy(y_sb[cols.start][:, :, i * BANK_M : (i + 1) * BANK_M], y_banks[c][:])
-            nc.sync.dma_start(y_rows[:, :, cols], y_sb[cols.start][:])
+                if cols is chunks[-1]:
+                    nc.sync.dma_start(
+                        y_rows[:, :, c * BANK_M : (c + 1) * BANK_M], y_sb[cols.start][:, :, i * BANK_M : (i + 1) * BANK_M]
+                    )
+            if cols is not chunks[-1]:
+                nc.sync.dma_start(y_rows[:, :, cols], y_sb[cols.start][:])
         for cols in chunks:
-            copy = nc.scalar.copy if cols.start == 0 else nc.vector.tensor_copy
-            copy(y_bf[:, cols, :], y_sb[cols.start][:].rearrange("p t m -> p m t"))
-            quantise("y", 0, y_bf, cols)
-            nc.sync.dma_start(out_words[:, cols], y_words[:, cols])
+            width = BANK_M if cols is chunks[-1] else TAIL_M
+            for m0 in range(0, TAIL_M, width):
+                part = slice(cols.start + m0, cols.start + m0 + width)
+                values = y_sb[cols.start][:, :, m0 : m0 + width]
+                nc.vector.tensor_copy(y_bf[:, part, :], values.rearrange("p t m -> p m t"))
+                quantise("y", 0, y_bf, part)
+            if cols is chunks[-2]:
+                nc.sync.dma_start(out_words[:, 0 : cols.stop], y_words[:, 0 : cols.stop])
+        nc.scalar.dma_start(out_words[:, chunks[-1]], y_words[:, chunks[-1]])
         for q in range(4):
             queue = nc.sync if q % 2 == 0 else nc.scalar
             queue.dma_start(out_2[0][4 * q : 4 * q + 4, :].bitcast(I32), y_scales[32 * q : 32 * q + 4, :].bitcast(I32))

@@ -21,9 +21,26 @@ PACK = 4
 PASSES = 2
 SLICES = PASSES * PACK
 HALF = 512
-BANK_M = 128
-TAIL_M = 256
-HW_MOVES = 6
+FIRST = 256
+CHUNK = 256
+KIB = 1024
+EDGE = 64
+
+AT_NOISE = 0
+AT_TAB0 = AT_NOISE + 32 * KIB - EDGE
+AT_PAGE1 = AT_TAB0 + EDGE
+AT_W1_RAW1 = AT_PAGE1 + 8 * KIB
+AT_FACTORS = AT_W1_RAW1 + 2 * KIB
+AT_WGS = AT_FACTORS + EDGE
+AT_TAB1 = AT_WGS + 16 * KIB
+AT_PAGE2 = AT_TAB1
+AT_W4_RAW = AT_PAGE2 + 8 * KIB
+AT_W4_SC_RAW = AT_W4_RAW + 4 * KIB
+AT_W3_RAW = AT_W4_SC_RAW + 512
+AT_HZ0 = AT_W3_RAW + 16 * KIB
+AT_HZ45 = AT_HZ0 + 16 * KIB
+AT_H67 = AT_HZ45 + 8 * KIB
+AT_END = AT_H67 + 8 * KIB
 
 
 def tile_list_packet_loss_concealer_kernel(
@@ -34,140 +51,152 @@ def tile_list_packet_loss_concealer_kernel(
     with ExitStack() as ctx:
         lists = ctx.enter_context(tc.tile_pool(name="lists", bufs=1))
         sb = ctx.enter_context(tc.tile_pool(name="sb", bufs=1))
+        placed = ctx.enter_context(tc.tile_pool(name="placed", bufs=1))
         psum = ctx.enter_context(tc.psum_pool(name="psum", bufs=1))
 
-        def alloc(shape, dtype, name, tag=None, bufs=1):
-            return sb.tile(shape, dtype, name=name, tag=tag or name, bufs=bufs, align_bytes=64)
+        def alloc(shape, dtype, name, tag=None):
+            return sb.tile(shape, dtype, name=name, tag=tag or name, align_bytes=64)
+
+        def place(shape, dtype, name, at):
+            return placed.tile(shape, dtype, name=name, tag=name, align_bytes=64, offset=at)
 
         idx = lists.tile([P, S // 16], U16, name="idx")
         idx2 = lists.tile([P, S // 16], U16, name="idx2")
         idx3 = lists.tile([P, M // 16], U16, name="idx3")
-        nc.sync.dma_start(idx[:], offs)
-        nc.sync.dma_start(idx2[:], offs2)
-        nc.sync.dma_start(idx3[:], offs3)
 
         tab_sc = alloc([P, T], U8, "tab_sc")
-        w1_sc_raw = alloc([P, H], U8, "w1_sc_raw", tag="page0")
+        w1_sc_raw = alloc([P, H], U8, "w1_sc_raw")
+        w1_halves = w1_words.rearrange("a p (b c) -> b p a c", b=PASSES)
+        w1_raw = [alloc([P, PASSES, H], U8, "w1_raw0"), None]
+        nc.sync.dma_start(idx[:], offs)
         nc.sync.dma_start(tab_sc[0:32, :].bitcast(I32), tab_scales.rearrange("a q t -> (a q) t").bitcast(I32))
         nc.sync.dma_start(w1_sc_raw[0:32, :].bitcast(I32), w1_scales.rearrange("a q c -> (a q) c").bitcast(I32))
+        nc.sync.dma_start(w1_raw[0][:].bitcast(I32), w1_halves[0].bitcast(I32))
+        nc.sync.dma_start(idx2[:], offs2)
+        nc.sync.dma_start(idx3[:], offs3)
+        tab_w = []
+        for a in range(PASSES):
+            t_w = place([P, T], I32, "tab_w%d" % a, (AT_TAB0, AT_TAB1)[a])
+            nc.sync.dma_start(t_w[:], tab_words[a].rearrange("p t i -> p (t i)").bitcast(I32))
+            tab_w.append(t_w)
         for rows in (tab_sc, w1_sc_raw):
             nc.vector.memset(rows[32:64, :].bitcast(I32), 0)
             nc.vector.memset(rows[64:128, :].bitcast(I32), 0)
-        w1_raw = alloc([P, PASSES, 2 * H], U8, "w1_raw", tag="page1")
-        nc.sync.dma_start(w1_raw[:].bitcast(I32), w1_words.rearrange("a p c -> p a c").bitcast(I32))
-        tab_w = []
-        for a in range(PASSES):
-            t_w = alloc([P, T], I32, "tab_w%d" % a, tag="big%d" % a)
-            nc.sync.dma_start(t_w[:], tab_words[a].rearrange("p t i -> p (t i)").bitcast(I32))
-            tab_w.append(t_w)
         planes = alloc([P, PASSES, S + H], U8, "planes")
-        nc.vector.memset(planes[:].rearrange("p a c -> p (a c)").bitcast(I32), 0)
+        nc.vector.memset(planes[:, 1, :].bitcast(I32), 0)
+        pages = [alloc([P, T2], F32, "page0"), None, None]
+        nc.vector.memset(pages[0][:], 0.0)
 
         picked_sc = alloc([P, S], U8, "picked_sc")
         nc.vector.tensor_copy(picked_sc[:], tab_sc[:].indirect(idx[:]))
-        staged = alloc([P, S + H], U8, "staged")
         nc.vector.tensor_copy(
-            staged[:, S : S + H].rearrange("p (b t m) -> p b t m", b=PASSES, t=PACK),
-            w1_sc_raw[:].rearrange("p (b m t) -> p b t m", b=PASSES, t=PACK),
+            planes[:, 0, S : S + H].rearrange("p (b t c i) -> p b c t i", b=PASSES, t=PACK, i=16),
+            w1_sc_raw[:].rearrange("p (b c i t) -> p b c t i", b=PASSES, t=PACK, i=16),
         )
-        nc.vector.tensor_copy(staged[:, 0:S].bitcast(I32), picked_sc[:].bitcast(I32))
-        for n_move in range(PASSES * 4):
-            a, q = divmod(n_move, 4)
-            queue = nc.sync if n_move < HW_MOVES else nc.gpsimd
+        nc.vector.tensor_copy(planes[:, 0, 0:S].bitcast(I32), picked_sc[:].bitcast(I32))
+        for a, q in [divmod(n_move, 4) for n_move in range(1, PASSES * 4)]:
             row = 16 * a + 4 * q
-            queue.dma_start(planes[32 * q : 32 * q + 4, a, :].bitcast(I32), staged[row : row + 4, :].bitcast(I32))
+            nc.sync.dma_start(planes[32 * q : 32 * q + 4, a, :].bitcast(I32), planes[row : row + 4, 0, :].bitcast(I32))
 
-        wgs_rows = wgs.rearrange("(i t) j -> i t j", t=PACK)
-        wgs_first = alloc([P, S], F32, "wgs_first", tag="picked_sc")
-        for q in range(4):
-            nc.sync.dma_start(wgs_first[32 * q : 32 * q + 32, :], wgs_rows[:, 0, :])
+        w1_w = {}
 
-        w1_w = []
-        for b in range(PASSES):
-            dealt = alloc([P, PASSES, 2 * HALF], U8, "w1_w%d" % b, tag="w1w%d" % b)
+        def deal_w1(b):
+            w1_w[b] = alloc([P, PASSES, H], U8, "w1_w%d" % b)
             nc.vector.tensor_copy(
-                dealt[:].bitcast(U16).rearrange("p a (t m) -> p a t m", t=PACK),
-                w1_raw[:].bitcast(U16)[:, :, b * HALF : (b + 1) * HALF].rearrange("p a (m t) -> p a t m", t=PACK),
+                w1_w[b][:].bitcast(U16).rearrange("p a (t c i) -> p a c t i", t=PACK, i=8),
+                w1_raw[b][:].bitcast(U16).rearrange("p a (c i t) -> p a c t i", t=PACK, i=8),
             )
-            w1_w.append(dealt)
 
-        v_first = alloc([P, S], U32, "v_first", tag="vw_then_noise")
+        deal_w1(0)
+
+        v_first = alloc([P, S], U32, "v_first")
         nc.vector.tensor_copy(v_first[:], tab_w[0][:].bitcast(U32).indirect(idx[:]))
         v_w = {(0, half): v_first[:, half * HALF : (half + 1) * HALF] for half in range(2)}
+        pages[1] = place([P, T2], F32, "page1", AT_PAGE1)
+        nc.vector.memset(pages[1][:], 0.0)
         for half in range(2):
-            picked = alloc([P, HALF], U32, "v_second%d" % half, tag=("vsc_then_w3", "v_then_w4")[half])
+            picked = alloc([P, HALF], U32, "v_second%d" % half)
             nc.vector.tensor_copy(picked[:], tab_w[1][:].bitcast(U32).indirect(idx[:, half * 32 : (half + 1) * 32]))
             v_w[1, half] = picked[:]
+        pages[2] = place([P, T2], F32, "page2", AT_PAGE2)
+        nc.gpsimd.memset(pages[2][:], 0.0)
 
-        pages = [alloc([P, T2], F32, "page%d" % i) for i in range(2)]
-        for page in pages:
-            nc.vector.memset(page[:], 0.0)
+        wgs_sb = place([P, PACK, S], F32, "wgs_sb", AT_WGS)
+        wgs_rows = wgs.rearrange("(i t) j -> i (t j)", t=PACK)
 
-        wgs_rest = alloc([P, PACK - 1, S], F32, "wgs_rest", tag="big0")
-        for q in range(4):
-            nc.sync.dma_start(wgs_rest[32 * q : 32 * q + 32, :, :], wgs_rows[:, 1:PACK, :])
-        noise_rows = noise.rearrange("(b p t) m -> b p t m", b=PASSES, t=PACK)
-        noise_sb = [alloc([P, PACK, M], F32, "noise0", tag="big1"), None]
-        for u in range(2):
-            nc.sync.dma_start(noise_sb[0][:, 2 * u : 2 * u + 2, :], noise_rows[0][:, 2 * u : 2 * u + 2, :])
-
-        h_sb = {}
-
-        def project(s):
-            b, t = divmod(s, PACK)
-            h_sb[s] = alloc([P, S], F32, "h%d" % s)
-            for half in range(2):
-                cols = slice(half * HALF, (half + 1) * HALF)
-                bank = psum.tile([P, HALF], F32, name="hbank%d_%d" % (s, half), tag="bank%d" % ((2 * s + half) % 8))
-                for a in range(PASSES):
-                    nc.tensor.matmul_mx(
-                        out=bank[:],
-                        lhsT=w1_w[b][:, a, 2 * P * t : 2 * P * (t + 1)].bitcast(FP4X4),
-                        lhsT_scale=planes[:, a, S + P * s : S + P * (s + 1)],
-                        rhs=v_w[a, half].bitcast(FP8X4),
-                        rhs_scale=planes[:, a, cols],
-                        start=(a == 0),
-                        stop=(a == PASSES - 1),
-                    )
-                nc.scalar.activation(h_sb[s][:, cols], bank[:], ACT.Square)
-
-        def scatter(s):
-            t = s % PACK
-            weight = wgs_first[:] if t == 0 else wgs_rest[:, t - 1, :]
-            page = pages[page_of(s)]
-            pieces = 2 if s == 0 else 1
-            width = S // pieces
-            for i in range(pieces):
-                cols = slice(i * width, (i + 1) * width)
-                nc.vector.tensor_tensor(
-                    page[:].indirect(idx2[:, i * width // 16 : (i + 1) * width // 16]),
-                    h_sb[s][:, cols], weight[:, cols], ALU.mult,
+        def load_wgs(start, stop):
+            for q in range(4):
+                nc.sync.dma_start(
+                    wgs_sb[32 * q : 32 * q + 32].rearrange("p t j -> p (t j)")[:, start:stop], wgs_rows[:, start:stop]
                 )
 
-        def page_of(s):
-            return s % 2 if s < SLICES - 1 else (s - 1) % 2
+        noise_sb = place([P, SLICES, M], F32, "noise_sb", AT_NOISE)
+        noise_rows = noise.rearrange("(b p t) m -> p b t m", b=PASSES, t=PACK)
 
-        z_pair = {}
-        z_bf, d_bf = {}, {}
-
-        def gather(s, cols):
-            b, t = divmod(s, PACK)
-            nc.vector.tensor_tensor(
-                z_pair[s // 2][:, s % 2, cols],
-                pages[page_of(s)][:].indirect(idx3[:, cols.start // 16 : cols.stop // 16]),
-                noise_sb[b][:, t, cols], ALU.add,
-            )
-
-        def bend_plane(s, cols):
-            b, t = divmod(s, PACK)
-            width = cols.stop - cols.start
-            tanh = alloc([P, width], F32, "tanh%d_%d" % (s, cols.start), tag=("vsc_then_w3", "w1w1")[(s + cols.start // TAIL_M) % 2])
-            nc.scalar.activation(tanh[:], z_pair[s // 2][:, s % 2, cols], ACT.Tanh, scale=bend_sb[:, b, t : t + 1])
-            nc.scalar.activation(d_bf[b][:, cols, t], tanh[:], ACT.Copy, scale=gain_sb[:, b, t : t + 1])
-
-        def round_pair(pair, cols, copy):
+        def load_noise(pair):
             b, u = divmod(pair, 2)
-            copy(z_bf[b][:, cols, 2 * u : 2 * u + 2], z_pair[pair][:, :, cols].rearrange("p e m -> p m e"))
+            nc.sync.dma_start(noise_sb[:, 2 * pair : 2 * pair + 2, :], noise_rows[:, b, 2 * u : 2 * u + 2, :])
+
+        load_wgs(0, FIRST)
+        load_wgs(FIRST, 2 * S)
+        w1_raw[1] = place([P, PASSES, H], U8, "w1_raw1", AT_W1_RAW1)
+        nc.sync.dma_start(w1_raw[1][:].bitcast(I32), w1_halves[1].bitcast(I32))
+        load_noise(0)
+        factors = place([P, 2, PASSES, PACK], F32, "factors", AT_FACTORS)
+        bend_sb, gain_sb = factors[:, 0], factors[:, 1]
+        nc.sync.dma_start(bend_sb, bend.rearrange("(b p t) -> p b t", b=PASSES, t=PACK))
+        nc.sync.dma_start(gain_sb, gain.rearrange("(b p t) -> p b t", b=PASSES, t=PACK))
+        load_wgs(2 * S, 4 * S)
+        for pair in range(1, 4):
+            load_noise(pair)
+        w3_raw = place([P, PASSES, PACK, N], F32, "w3_raw", AT_W3_RAW)
+        w3_rows = w3.rearrange("(b p j) n -> b p j n", b=PASSES, j=PACK)
+        for b in range(PASSES):
+            nc.sync.dma_start(w3_raw[:, b], w3_rows[b])
+        w4_raw = place([P, PASSES, N], I32, "w4_raw", AT_W4_RAW)
+        nc.sync.dma_start(w4_raw[:], w4_words.rearrange("a p c i -> p a (c i)").bitcast(I32))
+        w4_sc_raw = place([P, N], U8, "w4_sc_raw", AT_W4_SC_RAW)
+        nc.gpsimd.memset(w4_sc_raw[:].bitcast(I32), 0)
+        for q in range(4):
+            nc.sync.dma_start(w4_sc_raw[32 * q : 32 * q + 8, :].bitcast(I32), w4_scales[:, 4 * q : 4 * q + 4, :].bitcast(I32))
+
+        hz0 = place([P, PACK, S], F32, "hz0", AT_HZ0)
+        hz45 = place([P, 2, S], F32, "hz45", AT_HZ45)
+        h67 = place([P, 2, S], F32, "h67", AT_H67)
+        h_of = [hz0[:, t, :] for t in range(PACK)] + [hz45[:, 0, :], hz45[:, 1, :], h67[:, 0, :], h67[:, 1, :]]
+        z_of = h_of[:6] + h_of[2:4]
+        bank_count = [0]
+
+        def next_bank(shape, name):
+            bank = psum.tile(shape, F32, name=name, tag="bank%d" % (bank_count[0] % 8))
+            bank_count.append(bank_count.pop() + 1)
+            return bank
+
+        def project(s, cols, width):
+            b, t = divmod(s, PACK)
+            half, first = divmod(cols.start, HALF)
+            bank = next_bank([P, cols.stop - cols.start], "hbank%d_%d" % (s, cols.start))
+            for c0 in range(0, cols.stop - cols.start, width):
+                for a in (1, 0):
+                    nc.tensor.matmul_mx(
+                        out=bank[:, c0 : c0 + width],
+                        lhsT=w1_w[b][:, a, 2 * P * t : 2 * P * (t + 1)].bitcast(FP4X4),
+                        lhsT_scale=planes[:, a, S + P * s : S + P * (s + 1)],
+                        rhs=v_w[a, half][:, first + c0 : first + c0 + width].bitcast(FP8X4),
+                        rhs_scale=planes[:, a, cols.start + c0 : cols.start + c0 + width],
+                        start=(a == 1),
+                        stop=(a == 0),
+                    )
+            nc.scalar.activation(h_of[s][:, cols], bank[:], ACT.Square)
+
+        project(0, slice(0, FIRST), P)
+        project(0, slice(FIRST, HALF), P)
+        project(0, slice(HALF, S), HALF)
+        for s in range(1, SLICES):
+            if s == PACK:
+                deal_w1(1)
+            for half in range(2):
+                project(s, slice(half * HALF, (half + 1) * HALF), HALF)
 
         codes = {}
 
@@ -179,144 +208,154 @@ def tile_list_packet_loss_concealer_kernel(
                 in_=source[:, cols, :].rearrange("p m t -> p (m t)"),
             )
 
-        def second_weights():
-            w3_rows = w3.rearrange("(b p j) n -> b p j n", b=PASSES, j=PACK)
-            for b in range(PASSES):
-                raw = alloc([P, PACK, N], F32, "w3_raw%d" % b, tag=("vsc_then_w3", "w1w1")[b])
-                nc.sync.dma_start(raw[:], w3_rows[b])
-                grouped = alloc([P, N, PACK], BF16, "w3_bf%d" % b, tag="w3_bf%d" % b)
-                nc.scalar.copy(
-                    grouped[:].rearrange("p (t m) j -> p t m j", t=PACK),
-                    raw[:].rearrange("p j (m t) -> p t m j", t=PACK),
-                )
-                codes["w3", b] = (alloc([P, N], U32, "w3_w%d" % b), alloc([P, N], U8, "w3_sc%d" % b))
-                quantise("w3", b, grouped, slice(0, N))
-            w4_raw = alloc([P, PASSES, N], I32, "w4_raw", tag="v_then_w4")
-            nc.sync.dma_start(w4_raw[:], w4_words.rearrange("a p c i -> p a (c i)").bitcast(I32))
-            w4_sc_raw = planes[:, :, 0:N]
-            for q in range(4):
-                nc.sync.dma_start(
-                    planes[32 * q : 32 * q + 4, :, 0:N].bitcast(I32),
-                    w4_scales[:, 4 * q : 4 * q + 4, :].rearrange("a r c -> r a c").bitcast(I32),
-                )
-            return w4_raw[:], w4_sc_raw
+        for b in range(PASSES):
+            grouped = alloc([P, N, PACK], BF16, "w3_bf%d" % b)
+            nc.scalar.copy(
+                grouped[:].rearrange("p (t m) j -> p m t j", t=PACK),
+                w3_raw[:, b].rearrange("p j (m t) -> p m t j", t=PACK),
+            )
+            codes["w3", b] = (alloc([P, N], U32, "w3_w%d" % b), alloc([P, N], U8, "w3_sc%d" % b))
+            quantise("w3", b, grouped, slice(0, N))
+        w4_w = alloc([P, PASSES, N], I32, "w4_w")
+        w4_sc = alloc([P, N], U8, "w4_sc")
+        nc.vector.tensor_copy(
+            w4_w[:].rearrange("p a (t c i) -> p a c t i", t=PACK, i=4),
+            w4_raw[:].rearrange("p a (c i t) -> p a c t i", t=PACK, i=4),
+        )
+        nc.vector.tensor_copy(
+            w4_sc[:].rearrange("p (t c i) -> p c t i", t=PACK, i=16),
+            w4_sc_raw[:].rearrange("p (c i t) -> p c t i", t=PACK, i=16),
+        )
+        for b in range(PASSES):
+            codes["w4", b] = (w4_w[:, b, :], w4_sc[4 * b : P, :])
 
-        def deal_w4(w4_raw, w4_sc_raw):
-            w4_w = alloc([P, PASSES, N], I32, "w4_w", tag="h4")
-            w4_sc = alloc([P, PASSES, N], U8, "w4_sc", tag="h5")
-            for dealt, raw in ((w4_w, w4_raw), (w4_sc, w4_sc_raw)):
-                nc.vector.tensor_copy(
-                    dealt[:].rearrange("p a (t m) -> p a t m", t=PACK),
-                    raw.rearrange("p a (m t) -> p a t m", t=PACK),
-                )
-            for b in range(PASSES):
-                codes["w4", b] = (w4_w[:, b, :], w4_sc[:, b, :])
+        def page_of(s):
+            return pages[min(s, SLICES - 2) % 3]
 
+        def scatter(s, cols):
+            nc.vector.tensor_tensor(
+                page_of(s)[:].indirect(idx2[:, cols.start // 16 : cols.stop // 16]),
+                h_of[s][:, cols], wgs_sb[:, s % PACK, cols], ALU.mult,
+            )
+
+        def gather(s, cols):
+            nc.vector.tensor_tensor(
+                z_of[s][:, cols],
+                page_of(s)[:].indirect(idx3[:, cols.start // 16 : cols.stop // 16]),
+                noise_sb[:, s, cols], ALU.add,
+            )
+
+        z_bf = [alloc([P, M, PACK], BF16, "z_bf%d" % b) for b in range(PASSES)]
+        d_bf = [alloc([P, M, PACK], BF16, "d_bf%d" % b) for b in range(PASSES)]
+        tanh_count = [0]
+
+        def bend_plane(s, cols):
+            b, t = divmod(s, PACK)
+            tanh = alloc([P, cols.stop - cols.start], F32, "tanh%d_%d" % (s, cols.start), tag="tanh%d" % (tanh_count[0] % 2))
+            tanh_count.append(tanh_count.pop() + 1)
+            nc.scalar.activation(tanh[:], z_of[s][:, cols], ACT.Tanh, scale=bend_sb[:, b, t : t + 1])
+            nc.scalar.activation(d_bf[b][:, cols, t], tanh[:], ACT.Copy, scale=gain_sb[:, b, t : t + 1])
+
+        for name, b in (("z", 0), ("z", 1), ("d", 1)):
+            codes[name, b] = (alloc([P, M], U32, "%s_w%d" % (name, b)), alloc([P, M], U8, "%s_sc%d" % (name, b)))
+
+        pieces = [slice(0, 256), slice(256, 512), slice(512, 768), slice(768, 896), slice(896, 1024)]
         y_banks = {}
 
-        def multiply(weight, moving, b, c):
-            cols = slice(c * BANK_M, (c + 1) * BANK_M)
+        def multiply(weight, moving, b, cols):
             opens = b == 0 and moving == "z"
             closes = b == PASSES - 1 and moving == "d"
-            if opens:
-                y_banks[c] = psum.tile([P, PACK, BANK_M], F32, name="ybank%d" % c, tag="bank%d" % c)
-            for t in range(PACK):
-                n_cols = slice(t * P, (t + 1) * P)
-                nc.tensor.matmul_mx(
-                    out=y_banks[c][:, t, :],
-                    lhsT=codes[weight, b][0][:, n_cols].bitcast(FP8X4),
-                    lhsT_scale=codes[weight, b][1][:, n_cols],
-                    rhs=codes[moving, b][0][:, cols].bitcast(FP8X4),
-                    rhs_scale=codes[moving, b][1][:, cols],
-                    start=(opens and t == 0),
-                    stop=(closes and t == PACK - 1),
-                )
-
-        def banks_of(cols):
-            return range(cols.start // BANK_M, cols.stop // BANK_M)
-
-        def open_slice(s):
-            b, t = divmod(s, PACK)
-            if s % 2 == 0:
-                z_pair[s // 2] = alloc([P, 2, M], F32, "z_pair%d" % (s // 2), tag=("z_pair0", "z_pair1", "z_pair0", "z_bf0")[s // 2])
-            if t == 0:
-                z_bf[b] = alloc([P, M, PACK], BF16, "z_bf%d" % b)
-                d_bf[b] = alloc([P, M, PACK], BF16, "d_bf%d" % b)
-                for name in ("z", "d"):
-                    if (name, b) != ("d", 0):
-                        codes[name, b] = (alloc([P, M], U32, "%s_w%d" % (name, b)), alloc([P, M], U8, "%s_sc%d" % (name, b)))
+            for piece in pieces:
+                if piece.start < cols.start or piece.stop > cols.stop:
+                    continue
+                width = piece.stop - piece.start
+                per_bank = HALF // width
+                for t in range(PACK):
+                    u, e = divmod(t, per_bank)
+                    if opens and e == 0:
+                        y_banks[piece.start, u] = next_bank([P, per_bank, width], "ybank%d_%d" % (piece.start, u))
+                    n_cols = slice(t * P, (t + 1) * P)
+                    nc.tensor.matmul_mx(
+                        out=y_banks[piece.start, u][:, e, :],
+                        lhsT=codes[weight, b][0][:, n_cols].bitcast(FP8X4),
+                        lhsT_scale=codes[weight, b][1][:, n_cols],
+                        rhs=codes[moving, b][0][:, piece].bitcast(FP8X4),
+                        rhs_scale=codes[moving, b][1][:, piece],
+                        start=(opens and e == 0),
+                        stop=(closes and e == per_bank - 1),
+                    )
 
         everything = slice(0, M)
-        for s in range(SLICES):
-            project(s)
-        factors = alloc([P, 2, PASSES, PACK], F32, "factors", tag="w1w0")
-        bend_sb, gain_sb = factors[:, 0], factors[:, 1]
-        nc.sync.dma_start(bend_sb, bend.rearrange("(b p t) -> p b t", b=PASSES, t=PACK))
-        nc.sync.dma_start(gain_sb, gain.rearrange("(b p t) -> p b t", b=PASSES, t=PACK))
-        w4_loaded = second_weights()
-        noise_sb[1] = alloc([P, PACK, M], F32, "noise1", tag="vw_then_noise")
-        nc.sync.dma_start(noise_sb[1][:], noise_rows[1])
-        scatter(0)
-        for s in range(SLICES - 1):
-            if s + 1 < SLICES - 1:
-                scatter(s + 1)
-            if s == 4:
-                deal_w4(*w4_loaded)
-            open_slice(s)
+        last = SLICES - 1
+        scatter(0, slice(0, FIRST))
+        scatter(0, slice(FIRST, S))
+        for s in range(last):
+            if s + 1 < last:
+                scatter(s + 1, everything)
             gather(s, everything)
             bend_plane(s, everything)
-            if s % 2 == 1:
-                round_pair(s // 2, everything, nc.scalar.copy)
             if s == PACK - 1:
-                quantise("z", 0, z_bf[0], everything)
-                for c in banks_of(everything):
-                    multiply("w3", "z", 0, c)
+                nc.scalar.copy(z_bf[0][:], hz0[:].rearrange("p t m -> p m t"))
+            if s == PACK + 1:
+                nc.scalar.copy(z_bf[1][:, :, 0:2], hz45[:].rearrange("p e m -> p m e"))
+        quantise("z", 0, z_bf[0], everything)
+        multiply("w3", "z", 0, everything)
+        scatter(last, everything)
 
-        last = SLICES - 1
-        scatter(last)
-        chunks = [slice(c0, c0 + TAIL_M) for c0 in range(0, M, TAIL_M)]
+        codes["d", 0] = (place([P, M], U32, "d_w0", AT_H67), alloc([P, M], U8, "d_sc0"))
         y_rows = out_0.rearrange("(p t) m -> p t m", t=PACK)
         y_words = alloc([P, M], I32, "y_words")
         y_scales = alloc([P, M], U8, "y_scales")
         codes["y", 0] = (y_words, y_scales)
-        y_bf = alloc([P, M, PACK], BF16, "y_bf", tag="big1")
+        y_bf = place([P, M, PACK], BF16, "y_bf", AT_NOISE)
         out_words = out_1[0].rearrange("p m t -> p (m t)").bitcast(I32)
-        codes["d", 0] = (alloc([P, M], U32, "d_w0", tag="h%d" % last), alloc([P, M], U8, "d_sc0"))
-        for cols in chunks:
-            gather(last, cols)
-            bend_plane(last, cols)
-            quantise("d", 0, d_bf[0], cols)
-            for c in banks_of(cols):
-                multiply("w4", "d", 0, c)
-        for cols in chunks[2:]:
-            round_pair(last // 2, cols, nc.scalar.copy)
         y_sb = {}
-        for n_chunk, cols in enumerate(chunks):
-            if n_chunk < 2:
-                round_pair(last // 2, cols, nc.vector.tensor_copy)
+
+        def finish(cols):
             quantise("z", 1, z_bf[1], cols)
             quantise("d", 1, d_bf[1], cols)
-            y_sb[cols.start] = alloc([P, PACK, TAIL_M], F32, "y%d" % cols.start, tag="h%d" % n_chunk)
-            for i, c in enumerate(banks_of(cols)):
-                multiply("w3", "z", 1, c)
-                multiply("w4", "d", 1, c)
-                nc.scalar.copy(y_sb[cols.start][:, :, i * BANK_M : (i + 1) * BANK_M], y_banks[c][:])
-                if cols is chunks[-1]:
-                    nc.sync.dma_start(
-                        y_rows[:, :, c * BANK_M : (c + 1) * BANK_M], y_sb[cols.start][:, :, i * BANK_M : (i + 1) * BANK_M]
-                    )
-            if cols is not chunks[-1]:
-                nc.sync.dma_start(y_rows[:, :, cols], y_sb[cols.start][:])
-        for cols in chunks:
-            width = BANK_M if cols is chunks[-1] else TAIL_M
-            for m0 in range(0, TAIL_M, width):
-                part = slice(cols.start + m0, cols.start + m0 + width)
-                values = y_sb[cols.start][:, :, m0 : m0 + width]
-                nc.vector.tensor_copy(y_bf[:, part, :], values.rearrange("p t m -> p m t"))
-                quantise("y", 0, y_bf, part)
-            if cols is chunks[-2]:
-                nc.sync.dma_start(out_words[:, 0 : cols.stop], y_words[:, 0 : cols.stop])
-        nc.scalar.dma_start(out_words[:, chunks[-1]], y_words[:, chunks[-1]])
+            for piece in pieces:
+                if piece.start < cols.start or piece.stop > cols.stop:
+                    continue
+                multiply("w3", "z", 1, piece)
+                multiply("w4", "d", 1, piece)
+                width = piece.stop - piece.start
+                per_bank = HALF // width
+                y_sb[piece.start] = place([P, PACK, width], F32, "y%d" % piece.start, AT_W3_RAW + 16 * piece.start)
+                for u in range(PACK // per_bank):
+                    nc.scalar.copy(y_sb[piece.start][:, u * per_bank : (u + 1) * per_bank, :], y_banks[piece.start, u][:])
+                nc.sync.dma_start(y_rows[:, :, piece], y_sb[piece.start][:])
+
+        def round_y(piece):
+            nc.vector.tensor_copy(
+                y_bf[:, piece, :].rearrange("p (c i) t -> p c t i", i=4),
+                y_sb[piece.start][:].rearrange("p t (c i) -> p c t i", i=4),
+            )
+
+        def round_z(cols):
+            nc.vector.tensor_copy(z_bf[1][:, cols, 2:4], hz0[:, 2:4, cols].rearrange("p e m -> p m e"))
+
+        chunks = [slice(c0, c0 + CHUNK) for c0 in range(0, M, CHUNK)]
+        for k, cols in enumerate(chunks):
+            gather(last, cols)
+            bend_plane(last, cols)
+            if k >= 1:
+                round_z(chunks[k - 1])
+            quantise("d", 0, d_bf[0], cols)
+            multiply("w4", "d", 0, cols)
+            if k >= 2:
+                finish(chunks[k - 2])
+        round_z(chunks[-1])
+        finish(chunks[-2])
+        finish(chunks[-1])
+        round_y(pieces[0])
+        for i, piece in enumerate(pieces):
+            if i + 1 < len(pieces):
+                round_y(pieces[i + 1])
+            quantise("y", 0, y_bf, piece)
+            if i == 2:
+                nc.sync.dma_start(out_words[:, 0 : piece.stop], y_words[:, 0 : piece.stop])
+        nc.scalar.dma_start(out_words[:, pieces[2].stop : M], y_words[:, pieces[2].stop : M])
         for q in range(4):
             queue = nc.sync if q % 2 == 0 else nc.scalar
             queue.dma_start(out_2[0][4 * q : 4 * q + 4, :].bitcast(I32), y_scales[32 * q : 32 * q + 4, :].bitcast(I32))

@@ -26,21 +26,21 @@ CHUNK = 256
 KIB = 1024
 EDGE = 64
 
-AT_NOISE = 0
-AT_TAB0 = AT_NOISE + 32 * KIB - EDGE
+AT_W3_RAW = 0
+AT_TAB0 = AT_W3_RAW + 16 * KIB - EDGE
 AT_PAGE1 = AT_TAB0 + EDGE
 AT_W1_RAW1 = AT_PAGE1 + 8 * KIB
 AT_FACTORS = AT_W1_RAW1 + 2 * KIB
-AT_WGS = AT_FACTORS + EDGE
-AT_TAB1 = AT_WGS + 16 * KIB
-AT_PAGE2 = AT_TAB1
-AT_W4_RAW = AT_PAGE2 + 8 * KIB
+AT_WGS01 = AT_FACTORS + EDGE
+AT_NOISE = AT_WGS01 + 8 * KIB
+AT_TAB1 = AT_NOISE + 32 * KIB - EDGE
+AT_W4_RAW = AT_TAB1 + EDGE
 AT_W4_SC_RAW = AT_W4_RAW + 4 * KIB
-AT_W3_RAW = AT_W4_SC_RAW + 512
-AT_HZ0 = AT_W3_RAW + 16 * KIB
+AT_WGS23 = AT_W4_SC_RAW + 512
+AT_HZ0 = AT_TAB1 + 16 * KIB
 AT_HZ45 = AT_HZ0 + 16 * KIB
 AT_H67 = AT_HZ45 + 8 * KIB
-AT_END = AT_H67 + 8 * KIB
+AT_PAGE2 = AT_H67 + 8 * KIB
 
 
 def tile_list_packet_loss_concealer_kernel(
@@ -74,8 +74,16 @@ def tile_list_packet_loss_concealer_kernel(
         nc.sync.dma_start(w1_raw[0][:].bitcast(I32), w1_halves[0].bitcast(I32))
         nc.sync.dma_start(idx2[:], offs2)
         nc.sync.dma_start(idx3[:], offs3)
+        wgs_rows = wgs.rearrange("(i t) j -> i (t j)", t=PACK)
+        wgs0 = alloc([P, S], F32, "wgs0")
+
+        def load_wgs(tile, first, start, stop, quadrants=range(4)):
+            for q in quadrants:
+                nc.sync.dma_start(tile[32 * q : 32 * q + 32, start - first : stop - first], wgs_rows[:, start:stop])
+
         tab_w = []
         for a in range(PASSES):
+            load_wgs(wgs0, 0, 0, S, (range(0, 1), range(1, 4))[a])
             t_w = place([P, T], I32, "tab_w%d" % a, (AT_TAB0, AT_TAB1)[a])
             nc.sync.dma_start(t_w[:], tab_words[a].rearrange("p t i -> p (t i)").bitcast(I32))
             tab_w.append(t_w)
@@ -84,8 +92,9 @@ def tile_list_packet_loss_concealer_kernel(
             nc.vector.memset(rows[64:128, :].bitcast(I32), 0)
         planes = alloc([P, PASSES, S + H], U8, "planes")
         nc.vector.memset(planes[:, 1, :].bitcast(I32), 0)
-        pages = [alloc([P, T2], F32, "page0"), None, None]
-        nc.vector.memset(pages[0][:], 0.0)
+        pages = [alloc([P, T2], F32, "page0"), None, place([P, T2], F32, "page2", AT_PAGE2)]
+        nc.gpsimd.memset(pages[0][:], 0.0)
+        nc.gpsimd.memset(pages[2][:], 0.0)
 
         picked_sc = alloc([P, S], U8, "picked_sc")
         nc.vector.tensor_copy(picked_sc[:], tab_sc[:].indirect(idx[:]))
@@ -118,17 +127,17 @@ def tile_list_packet_loss_concealer_kernel(
             picked = alloc([P, HALF], U32, "v_second%d" % half)
             nc.vector.tensor_copy(picked[:], tab_w[1][:].bitcast(U32).indirect(idx[:, half * 32 : (half + 1) * 32]))
             v_w[1, half] = picked[:]
-        pages[2] = place([P, T2], F32, "page2", AT_PAGE2)
-        nc.gpsimd.memset(pages[2][:], 0.0)
 
-        wgs_sb = place([P, PACK, S], F32, "wgs_sb", AT_WGS)
-        wgs_rows = wgs.rearrange("(i t) j -> i (t j)", t=PACK)
+        wgs1 = place([P, S], F32, "wgs1", AT_WGS01)
+        wgs23 = place([P, 2 * S], F32, "wgs23", AT_WGS23)
 
-        def load_wgs(start, stop):
-            for q in range(4):
-                nc.sync.dma_start(
-                    wgs_sb[32 * q : 32 * q + 32].rearrange("p t j -> p (t j)")[:, start:stop], wgs_rows[:, start:stop]
-                )
+        def weights(s, cols):
+            start, stop = (s % PACK) * S + cols.start, (s % PACK) * S + cols.stop
+            if stop <= S:
+                return wgs0[:, start:stop]
+            if stop <= 2 * S:
+                return wgs1[:, start - S : stop - S]
+            return wgs23[:, start - 2 * S : stop - 2 * S]
 
         noise_sb = place([P, SLICES, M], F32, "noise_sb", AT_NOISE)
         noise_rows = noise.rearrange("(b p t) m -> p b t m", b=PASSES, t=PACK)
@@ -137,26 +146,25 @@ def tile_list_packet_loss_concealer_kernel(
             b, u = divmod(pair, 2)
             nc.sync.dma_start(noise_sb[:, 2 * pair : 2 * pair + 2, :], noise_rows[:, b, 2 * u : 2 * u + 2, :])
 
-        load_wgs(0, FIRST)
-        load_wgs(FIRST, 2 * S)
         w1_raw[1] = place([P, PASSES, H], U8, "w1_raw1", AT_W1_RAW1)
         nc.sync.dma_start(w1_raw[1][:].bitcast(I32), w1_halves[1].bitcast(I32))
-        load_noise(0)
-        factors = place([P, 2, PASSES, PACK], F32, "factors", AT_FACTORS)
-        bend_sb, gain_sb = factors[:, 0], factors[:, 1]
-        nc.sync.dma_start(bend_sb, bend.rearrange("(b p t) -> p b t", b=PASSES, t=PACK))
-        nc.sync.dma_start(gain_sb, gain.rearrange("(b p t) -> p b t", b=PASSES, t=PACK))
-        load_wgs(2 * S, 4 * S)
-        for pair in range(1, 4):
-            load_noise(pair)
+        load_wgs(wgs1, S, S, 2 * S)
         w3_raw = place([P, PASSES, PACK, N], F32, "w3_raw", AT_W3_RAW)
         w3_rows = w3.rearrange("(b p j) n -> b p j n", b=PASSES, j=PACK)
         for b in range(PASSES):
             nc.sync.dma_start(w3_raw[:, b], w3_rows[b])
+        factors = place([P, 2, PASSES, PACK], F32, "factors", AT_FACTORS)
+        bend_sb, gain_sb = factors[:, 0], factors[:, 1]
+        nc.sync.dma_start(bend_sb, bend.rearrange("(b p t) -> p b t", b=PASSES, t=PACK))
+        nc.sync.dma_start(gain_sb, gain.rearrange("(b p t) -> p b t", b=PASSES, t=PACK))
+        load_noise(0)
+        load_wgs(wgs23, 2 * S, 2 * S, 4 * S)
+        for pair in range(1, 4):
+            load_noise(pair)
         w4_raw = place([P, PASSES, N], I32, "w4_raw", AT_W4_RAW)
         nc.sync.dma_start(w4_raw[:], w4_words.rearrange("a p c i -> p a (c i)").bitcast(I32))
         w4_sc_raw = place([P, N], U8, "w4_sc_raw", AT_W4_SC_RAW)
-        nc.gpsimd.memset(w4_sc_raw[:].bitcast(I32), 0)
+        nc.vector.memset(w4_sc_raw[:].bitcast(I32), 0)
         for q in range(4):
             nc.sync.dma_start(w4_sc_raw[32 * q : 32 * q + 8, :].bitcast(I32), w4_scales[:, 4 * q : 4 * q + 4, :].bitcast(I32))
 
@@ -208,26 +216,34 @@ def tile_list_packet_loss_concealer_kernel(
                 in_=source[:, cols, :].rearrange("p m t -> p (m t)"),
             )
 
+        w3_bf = [alloc([P, N, PACK], BF16, "w3_bf%d" % b) for b in range(PASSES)]
         for b in range(PASSES):
-            grouped = alloc([P, N, PACK], BF16, "w3_bf%d" % b)
             nc.scalar.copy(
-                grouped[:].rearrange("p (t m) j -> p m t j", t=PACK),
+                w3_bf[b][:].rearrange("p (t m) j -> p m t j", t=PACK),
                 w3_raw[:, b].rearrange("p j (m t) -> p m t j", t=PACK),
             )
-            codes["w3", b] = (alloc([P, N], U32, "w3_w%d" % b), alloc([P, N], U8, "w3_sc%d" % b))
-            quantise("w3", b, grouped, slice(0, N))
-        w4_w = alloc([P, PASSES, N], I32, "w4_w")
-        w4_sc = alloc([P, N], U8, "w4_sc")
-        nc.vector.tensor_copy(
-            w4_w[:].rearrange("p a (t c i) -> p a c t i", t=PACK, i=4),
-            w4_raw[:].rearrange("p a (c i t) -> p a c t i", t=PACK, i=4),
-        )
-        nc.vector.tensor_copy(
-            w4_sc[:].rearrange("p (t c i) -> p c t i", t=PACK, i=16),
-            w4_sc_raw[:].rearrange("p (c i t) -> p c t i", t=PACK, i=16),
-        )
-        for b in range(PASSES):
-            codes["w4", b] = (w4_w[:, b, :], w4_sc[4 * b : P, :])
+
+        def quantise_w3():
+            for b in range(PASSES):
+                codes["w3", b] = (
+                    place([P, N], U32, "w3_w%d" % b, AT_PAGE1 + 2 * KIB * b),
+                    place([P, N], U8, "w3_sc%d" % b, AT_PAGE1 + 4 * KIB + N * b),
+                )
+                quantise("w3", b, w3_bf[b], slice(0, N))
+
+        def deal_w4():
+            w4_w = place([P, PASSES, N], I32, "w4_w", AT_PAGE2)
+            w4_sc = place([P, N], U8, "w4_sc", AT_PAGE2 + 4 * KIB)
+            nc.vector.tensor_copy(
+                w4_w[:].rearrange("p a (t c i) -> p a c t i", t=PACK, i=4),
+                w4_raw[:].rearrange("p a (c i t) -> p a c t i", t=PACK, i=4),
+            )
+            nc.vector.tensor_copy(
+                w4_sc[:].rearrange("p (t c i) -> p c t i", t=PACK, i=16),
+                w4_sc_raw[:].rearrange("p (c i t) -> p c t i", t=PACK, i=16),
+            )
+            for b in range(PASSES):
+                codes["w4", b] = (w4_w[:, b, :], w4_sc[4 * b : P, :])
 
         def page_of(s):
             return pages[min(s, SLICES - 2) % 3]
@@ -235,7 +251,7 @@ def tile_list_packet_loss_concealer_kernel(
         def scatter(s, cols):
             nc.vector.tensor_tensor(
                 page_of(s)[:].indirect(idx2[:, cols.start // 16 : cols.stop // 16]),
-                h_of[s][:, cols], wgs_sb[:, s % PACK, cols], ALU.mult,
+                h_of[s][:, cols], weights(s, cols), ALU.mult,
             )
 
         def gather(s, cols):
@@ -292,6 +308,8 @@ def tile_list_packet_loss_concealer_kernel(
         for s in range(last):
             if s + 1 < last:
                 scatter(s + 1, everything)
+            if s == PACK + 1:
+                quantise_w3()
             gather(s, everything)
             bend_plane(s, everything)
             if s == PACK - 1:
@@ -300,6 +318,7 @@ def tile_list_packet_loss_concealer_kernel(
                 nc.scalar.copy(z_bf[1][:, :, 0:2], hz45[:].rearrange("p e m -> p m e"))
         quantise("z", 0, z_bf[0], everything)
         multiply("w3", "z", 0, everything)
+        deal_w4()
         scatter(last, everything)
 
         codes["d", 0] = (place([P, M], U32, "d_w0", AT_H67), alloc([P, M], U8, "d_sc0"))

@@ -28,19 +28,25 @@ EDGE = 64
 
 AT_W3_RAW = 0
 AT_TAB0 = AT_W3_RAW + 16 * KIB - EDGE
-AT_PAGE1 = AT_TAB0 + EDGE
-AT_W1_RAW1 = AT_PAGE1 + 8 * KIB
-AT_FACTORS = AT_W1_RAW1 + 2 * KIB
-AT_WGS01 = AT_FACTORS + EDGE
-AT_NOISE = AT_WGS01 + 8 * KIB
-AT_TAB1 = AT_NOISE + 32 * KIB - EDGE
-AT_W4_RAW = AT_TAB1 + EDGE
-AT_W4_SC_RAW = AT_W4_RAW + 4 * KIB
-AT_WGS23 = AT_W4_SC_RAW + 512
-AT_HZ0 = AT_TAB1 + 16 * KIB
+AT_FACTORS = AT_TAB0 + EDGE
+AT_WGS1 = AT_FACTORS + EDGE
+AT_NOISE3 = AT_WGS1 + 4 * KIB
+AT_NOISE4 = AT_NOISE3 + 4 * KIB
+AT_NOISE012 = AT_NOISE4 + 4 * KIB
+AT_WGS23 = AT_NOISE012 + 12 * KIB
+AT_TAB1 = AT_WGS23 + 8 * KIB - EDGE
+AT_NOISE5 = AT_TAB1 + EDGE
+AT_NOISE6 = AT_NOISE5 + 4 * KIB
+AT_NOISE_LAST = AT_NOISE6 + 4 * KIB
+AT_W4_SC_RAW = AT_NOISE_LAST + 4 * KIB
+AT_PAGE1 = AT_W4_SC_RAW + 512
+AT_PAGE2 = AT_PAGE1 + 8 * KIB
+AT_W1_W0 = AT_PAGE2
+AT_HZ0 = AT_PAGE2 + 8 * KIB
 AT_HZ45 = AT_HZ0 + 16 * KIB
 AT_H67 = AT_HZ45 + 8 * KIB
-AT_PAGE2 = AT_H67 + 8 * KIB
+AT_TANH = AT_H67 + 8 * KIB
+AT_Y = AT_TANH - 512
 
 
 def tile_list_packet_loss_concealer_kernel(
@@ -66,12 +72,11 @@ def tile_list_packet_loss_concealer_kernel(
 
         tab_sc = alloc([P, T], U8, "tab_sc")
         w1_sc_raw = alloc([P, H], U8, "w1_sc_raw")
-        w1_halves = w1_words.rearrange("a p (b c) -> b p a c", b=PASSES)
-        w1_raw = [alloc([P, PASSES, H], U8, "w1_raw0"), None]
+        w1_raw = alloc([P, PASSES, 2 * H], U8, "w1_raw")
         nc.sync.dma_start(idx[:], offs)
         nc.sync.dma_start(tab_sc[0:32, :].bitcast(I32), tab_scales.rearrange("a q t -> (a q) t").bitcast(I32))
         nc.sync.dma_start(w1_sc_raw[0:32, :].bitcast(I32), w1_scales.rearrange("a q c -> (a q) c").bitcast(I32))
-        nc.sync.dma_start(w1_raw[0][:].bitcast(I32), w1_halves[0].bitcast(I32))
+        nc.sync.dma_start(w1_raw[:].bitcast(I32), w1_words.rearrange("a p c -> p a c").bitcast(I32))
         nc.sync.dma_start(idx2[:], offs2)
         nc.sync.dma_start(idx3[:], offs3)
         wgs_rows = wgs.rearrange("(i t) j -> i (t j)", t=PACK)
@@ -92,9 +97,8 @@ def tile_list_packet_loss_concealer_kernel(
             nc.vector.memset(rows[64:128, :].bitcast(I32), 0)
         planes = alloc([P, PASSES, S + H], U8, "planes")
         nc.vector.memset(planes[:, 1, :].bitcast(I32), 0)
-        pages = [alloc([P, T2], F32, "page0"), None, place([P, T2], F32, "page2", AT_PAGE2)]
-        nc.gpsimd.memset(pages[0][:], 0.0)
-        nc.gpsimd.memset(pages[2][:], 0.0)
+        pages = [alloc([P, T2], F32, "page0"), None, None]
+        nc.vector.memset(pages[0][:], 0.0)
 
         picked_sc = alloc([P, S], U8, "picked_sc")
         nc.vector.tensor_copy(picked_sc[:], tab_sc[:].indirect(idx[:]))
@@ -110,25 +114,27 @@ def tile_list_packet_loss_concealer_kernel(
         w1_w = {}
 
         def deal_w1(b):
-            w1_w[b] = alloc([P, PASSES, H], U8, "w1_w%d" % b)
+            w1_w[b] = place([P, PASSES, H], U8, "w1_w0", AT_W1_W0) if b == 0 else alloc([P, PASSES, H], U8, "w1_w1")
             nc.vector.tensor_copy(
                 w1_w[b][:].bitcast(U16).rearrange("p a (t c i) -> p a c t i", t=PACK, i=8),
-                w1_raw[b][:].bitcast(U16).rearrange("p a (c i t) -> p a c t i", t=PACK, i=8),
+                w1_raw[:, :, b * H : (b + 1) * H].bitcast(U16).rearrange("p a (c i t) -> p a c t i", t=PACK, i=8),
             )
 
         deal_w1(0)
+        deal_w1(1)
 
         v_first = alloc([P, S], U32, "v_first")
         nc.vector.tensor_copy(v_first[:], tab_w[0][:].bitcast(U32).indirect(idx[:]))
         v_w = {(0, half): v_first[:, half * HALF : (half + 1) * HALF] for half in range(2)}
-        pages[1] = place([P, T2], F32, "page1", AT_PAGE1)
-        nc.vector.memset(pages[1][:], 0.0)
         for half in range(2):
             picked = alloc([P, HALF], U32, "v_second%d" % half)
             nc.vector.tensor_copy(picked[:], tab_w[1][:].bitcast(U32).indirect(idx[:, half * 32 : (half + 1) * 32]))
             v_w[1, half] = picked[:]
 
-        wgs1 = place([P, S], F32, "wgs1", AT_WGS01)
+        pages[1] = place([P, T2], F32, "page1", AT_PAGE1)
+        nc.gpsimd.memset(pages[1][:], 0.0)
+
+        wgs1 = place([P, S], F32, "wgs1", AT_WGS1)
         wgs23 = place([P, 2 * S], F32, "wgs23", AT_WGS23)
 
         def weights(s, cols):
@@ -139,15 +145,16 @@ def tile_list_packet_loss_concealer_kernel(
                 return wgs1[:, start - S : stop - S]
             return wgs23[:, start - 2 * S : stop - 2 * S]
 
-        noise_sb = place([P, SLICES, M], F32, "noise_sb", AT_NOISE)
         noise_rows = noise.rearrange("(b p t) m -> p b t m", b=PASSES, t=PACK)
+        noise_of = {}
 
-        def load_noise(pair):
-            b, u = divmod(pair, 2)
-            nc.sync.dma_start(noise_sb[:, 2 * pair : 2 * pair + 2, :], noise_rows[:, b, 2 * u : 2 * u + 2, :])
+        def load_noise(first, count, at):
+            b, t = divmod(first, PACK)
+            tile = place([P, count, M], F32, "noise%d" % first, at)
+            nc.sync.dma_start(tile[:], noise_rows[:, b, t : t + count, :])
+            for i in range(count):
+                noise_of[first + i] = tile[:, i, :]
 
-        w1_raw[1] = place([P, PASSES, H], U8, "w1_raw1", AT_W1_RAW1)
-        nc.sync.dma_start(w1_raw[1][:].bitcast(I32), w1_halves[1].bitcast(I32))
         load_wgs(wgs1, S, S, 2 * S)
         w3_raw = place([P, PASSES, PACK, N], F32, "w3_raw", AT_W3_RAW)
         w3_rows = w3.rearrange("(b p j) n -> b p j n", b=PASSES, j=PACK)
@@ -157,11 +164,18 @@ def tile_list_packet_loss_concealer_kernel(
         bend_sb, gain_sb = factors[:, 0], factors[:, 1]
         nc.sync.dma_start(bend_sb, bend.rearrange("(b p t) -> p b t", b=PASSES, t=PACK))
         nc.sync.dma_start(gain_sb, gain.rearrange("(b p t) -> p b t", b=PASSES, t=PACK))
-        load_noise(0)
+        load_noise(0, 3, AT_NOISE012)
+        load_noise(3, 1, AT_NOISE3)
+        load_noise(4, 1, AT_NOISE4)
         load_wgs(wgs23, 2 * S, 2 * S, 4 * S)
-        for pair in range(1, 4):
-            load_noise(pair)
-        w4_raw = place([P, PASSES, N], I32, "w4_raw", AT_W4_RAW)
+        load_noise(5, 1, AT_NOISE5)
+        load_noise(6, 1, AT_NOISE6)
+        chunks = [slice(c0, c0 + CHUNK) for c0 in range(0, M, CHUNK)]
+        noise_last = {}
+        for cols in chunks:
+            noise_last[cols.start] = place([P, CHUNK], F32, "noise_last%d" % cols.start, AT_NOISE_LAST + 4 * cols.start)
+            nc.sync.dma_start(noise_last[cols.start][:], noise_rows[:, PASSES - 1, PACK - 1, cols])
+        w4_raw = alloc([P, PASSES, N], I32, "w4_raw", tag="w1_raw")
         nc.sync.dma_start(w4_raw[:], w4_words.rearrange("a p c i -> p a (c i)").bitcast(I32))
         w4_sc_raw = place([P, N], U8, "w4_sc_raw", AT_W4_SC_RAW)
         nc.vector.memset(w4_sc_raw[:].bitcast(I32), 0)
@@ -201,10 +215,11 @@ def tile_list_packet_loss_concealer_kernel(
         project(0, slice(FIRST, HALF), P)
         project(0, slice(HALF, S), HALF)
         for s in range(1, SLICES):
-            if s == PACK:
-                deal_w1(1)
             for half in range(2):
                 project(s, slice(half * HALF, (half + 1) * HALF), HALF)
+
+        pages[2] = place([P, T2], F32, "page2", AT_PAGE2)
+        nc.gpsimd.memset(pages[2][:], 0.0)
 
         codes = {}
 
@@ -223,17 +238,14 @@ def tile_list_packet_loss_concealer_kernel(
                 w3_raw[:, b].rearrange("p j (m t) -> p m t j", t=PACK),
             )
 
-        def quantise_w3():
-            for b in range(PASSES):
-                codes["w3", b] = (
-                    place([P, N], U32, "w3_w%d" % b, AT_PAGE1 + 2 * KIB * b),
-                    place([P, N], U8, "w3_sc%d" % b, AT_PAGE1 + 4 * KIB + N * b),
-                )
-                quantise("w3", b, w3_bf[b], slice(0, N))
+        def quantise_w3(b):
+            at = (AT_NOISE3, AT_NOISE4)[b]
+            codes["w3", b] = (place([P, N], U32, "w3_w%d" % b, at), place([P, N], U8, "w3_sc%d" % b, at + 2 * KIB))
+            quantise("w3", b, w3_bf[b], slice(0, N))
 
         def deal_w4():
-            w4_w = place([P, PASSES, N], I32, "w4_w", AT_PAGE2)
-            w4_sc = place([P, N], U8, "w4_sc", AT_PAGE2 + 4 * KIB)
+            w4_w = place([P, PASSES, N], I32, "w4_w", AT_NOISE5)
+            w4_sc = alloc([P, N], U8, "w4_sc", tag="w1_sc_raw")
             nc.vector.tensor_copy(
                 w4_w[:].rearrange("p a (t c i) -> p a c t i", t=PACK, i=4),
                 w4_raw[:].rearrange("p a (c i t) -> p a c t i", t=PACK, i=4),
@@ -258,19 +270,21 @@ def tile_list_packet_loss_concealer_kernel(
             nc.vector.tensor_tensor(
                 z_of[s][:, cols],
                 page_of(s)[:].indirect(idx3[:, cols.start // 16 : cols.stop // 16]),
-                noise_sb[:, s, cols], ALU.add,
+                noise_of[s][:, cols] if s < SLICES - 1 else noise_last[cols.start][:], ALU.add,
             )
 
         z_bf = [alloc([P, M, PACK], BF16, "z_bf%d" % b) for b in range(PASSES)]
         d_bf = [alloc([P, M, PACK], BF16, "d_bf%d" % b) for b in range(PASSES)]
-        tanh_count = [0]
 
-        def bend_plane(s, cols):
+        tanh_sb = place([P, M], F32, "tanh_sb", AT_TANH)
+
+        def bend_plane(s, pieces_of_m):
             b, t = divmod(s, PACK)
-            tanh = alloc([P, cols.stop - cols.start], F32, "tanh%d_%d" % (s, cols.start), tag="tanh%d" % (tanh_count[0] % 2))
-            tanh_count.append(tanh_count.pop() + 1)
-            nc.scalar.activation(tanh[:], z_of[s][:, cols], ACT.Tanh, scale=bend_sb[:, b, t : t + 1])
-            nc.scalar.activation(d_bf[b][:, cols, t], tanh[:], ACT.Copy, scale=gain_sb[:, b, t : t + 1])
+            tanh = z_of[s + 1] if s == SLICES - 2 else tanh_sb[:]
+            for cols in pieces_of_m:
+                nc.scalar.activation(tanh[:, cols], z_of[s][:, cols], ACT.Tanh, scale=bend_sb[:, b, t : t + 1])
+            for cols in pieces_of_m:
+                nc.scalar.activation(d_bf[b][:, cols, t], tanh[:, cols], ACT.Copy, scale=gain_sb[:, b, t : t + 1])
 
         for name, b in (("z", 0), ("z", 1), ("d", 1)):
             codes[name, b] = (alloc([P, M], U32, "%s_w%d" % (name, b)), alloc([P, M], U8, "%s_sc%d" % (name, b)))
@@ -278,9 +292,9 @@ def tile_list_packet_loss_concealer_kernel(
         pieces = [slice(0, 256), slice(256, 512), slice(512, 768), slice(768, 896), slice(896, 1024)]
         y_banks = {}
 
-        def multiply(weight, moving, b, cols):
+        def multiply(weight, moving, b, cols, words_from=0):
             opens = b == 0 and moving == "z"
-            closes = b == PASSES - 1 and moving == "d"
+            closes = b == PASSES - 1 and moving == "z"
             for piece in pieces:
                 if piece.start < cols.start or piece.stop > cols.stop:
                     continue
@@ -295,7 +309,7 @@ def tile_list_packet_loss_concealer_kernel(
                         out=y_banks[piece.start, u][:, e, :],
                         lhsT=codes[weight, b][0][:, n_cols].bitcast(FP8X4),
                         lhsT_scale=codes[weight, b][1][:, n_cols],
-                        rhs=codes[moving, b][0][:, piece].bitcast(FP8X4),
+                        rhs=codes[moving, b][0][:, piece.start - words_from : piece.stop - words_from].bitcast(FP8X4),
                         rhs_scale=codes[moving, b][1][:, piece],
                         start=(opens and e == 0),
                         stop=(closes and e == per_bank - 1),
@@ -306,44 +320,58 @@ def tile_list_packet_loss_concealer_kernel(
         scatter(0, slice(0, FIRST))
         scatter(0, slice(FIRST, S))
         for s in range(last):
-            if s + 1 < last:
+            if s + 1 < PACK:
                 scatter(s + 1, everything)
-            if s == PACK + 1:
-                quantise_w3()
+            if s >= PACK:
+                scatter(s, everything)
+                if s - PACK < PASSES:
+                    quantise_w3(s - PACK)
+                else:
+                    deal_w4()
             gather(s, everything)
-            bend_plane(s, everything)
-            if s == PACK - 1:
-                nc.scalar.copy(z_bf[0][:], hz0[:].rearrange("p t m -> p m t"))
-            if s == PACK + 1:
-                nc.scalar.copy(z_bf[1][:, :, 0:2], hz45[:].rearrange("p e m -> p m e"))
+            bend_plane(s, [slice(0, HALF), slice(HALF, M)])
+            if s % 2 == 1:
+                b, u = divmod(s // 2, 2)
+                pair = hz0[:, 2 * u : 2 * u + 2, :] if b == 0 else hz45[:]
+                nc.scalar.copy(z_bf[b][:, :, 2 * u : 2 * u + 2], pair.rearrange("p e m -> p m e"))
         quantise("z", 0, z_bf[0], everything)
         multiply("w3", "z", 0, everything)
-        deal_w4()
         scatter(last, everything)
 
-        codes["d", 0] = (place([P, M], U32, "d_w0", AT_H67), alloc([P, M], U8, "d_sc0"))
+        d_sc0 = alloc([P, M], U8, "d_sc0")
+
+        def first_d(cols):
+            words = place([P, CHUNK], U32, "d_w0_%d" % cols.start, AT_NOISE_LAST + 4 * cols.start)
+            nc.vector.quantize_mx(
+                out=words[:].bitcast(FP8X4), scales=d_sc0[:, cols], in_=d_bf[0][:, cols, :].rearrange("p m t -> p (m t)")
+            )
+            codes["d", 0] = (words, d_sc0)
+            multiply("w4", "d", 0, cols, cols.start)
+
         y_rows = out_0.rearrange("(p t) m -> p t m", t=PACK)
         y_words = alloc([P, M], I32, "y_words")
         y_scales = alloc([P, M], U8, "y_scales")
         codes["y", 0] = (y_words, y_scales)
-        y_bf = place([P, M, PACK], BF16, "y_bf", AT_NOISE)
+        y_bf = place([P, M, PACK], BF16, "y_bf", AT_NOISE012)
         out_words = out_1[0].rearrange("p m t -> p (m t)").bitcast(I32)
         y_sb = {}
 
         def finish(cols):
-            quantise("z", 1, z_bf[1], cols)
             quantise("d", 1, d_bf[1], cols)
+            quantise("z", 1, z_bf[1], cols)
             for piece in pieces:
                 if piece.start < cols.start or piece.stop > cols.stop:
                     continue
-                multiply("w3", "z", 1, piece)
                 multiply("w4", "d", 1, piece)
-                width = piece.stop - piece.start
-                per_bank = HALF // width
-                y_sb[piece.start] = place([P, PACK, width], F32, "y%d" % piece.start, AT_W3_RAW + 16 * piece.start)
-                for u in range(PACK // per_bank):
-                    nc.scalar.copy(y_sb[piece.start][:, u * per_bank : (u + 1) * per_bank, :], y_banks[piece.start, u][:])
-                nc.sync.dma_start(y_rows[:, :, piece], y_sb[piece.start][:])
+                multiply("w3", "z", 1, piece)
+
+        def store_y(piece):
+            width = piece.stop - piece.start
+            per_bank = HALF // width
+            y_sb[piece.start] = place([P, PACK, width], F32, "y%d" % piece.start, (AT_Y if piece.start < HALF else AT_W3_RAW) + 16 * piece.start)
+            for u in range(PACK // per_bank):
+                nc.scalar.copy(y_sb[piece.start][:, u * per_bank : (u + 1) * per_bank, :], y_banks[piece.start, u][:])
+            nc.sync.dma_start(y_rows[:, :, piece], y_sb[piece.start][:])
 
         def round_y(piece):
             nc.vector.tensor_copy(
@@ -354,19 +382,19 @@ def tile_list_packet_loss_concealer_kernel(
         def round_z(cols):
             nc.vector.tensor_copy(z_bf[1][:, cols, 2:4], hz0[:, 2:4, cols].rearrange("p e m -> p m e"))
 
-        chunks = [slice(c0, c0 + CHUNK) for c0 in range(0, M, CHUNK)]
-        for k, cols in enumerate(chunks):
-            gather(last, cols)
-            bend_plane(last, cols)
+        gather(last, chunks[0])
+        bend_plane(last, chunks[0:1])
+        for k in range(len(chunks) + 1):
+            if k + 1 < len(chunks):
+                gather(last, chunks[k + 1])
+                bend_plane(last, chunks[k + 1 : k + 2])
             if k >= 1:
-                round_z(chunks[k - 1])
-            quantise("d", 0, d_bf[0], cols)
-            multiply("w4", "d", 0, cols)
-            if k >= 2:
-                finish(chunks[k - 2])
-        round_z(chunks[-1])
-        finish(chunks[-2])
-        finish(chunks[-1])
+                finish(chunks[k - 1])
+            if k < len(chunks):
+                first_d(chunks[k])
+                round_z(chunks[k])
+        for piece in pieces:
+            store_y(piece)
         round_y(pieces[0])
         for i, piece in enumerate(pieces):
             if i + 1 < len(pieces):

@@ -29,20 +29,20 @@ EDGE = 64
 AT_W3_RAW = 0
 AT_TAB0 = AT_W3_RAW + 16 * KIB - EDGE
 AT_FACTORS = AT_TAB0 + EDGE
-AT_WGS1 = AT_FACTORS + EDGE
-AT_NOISE3 = AT_WGS1 + 4 * KIB
+AT_PAGE2 = AT_FACTORS + EDGE
+AT_WGS01 = AT_PAGE2 + 8 * KIB
+AT_NOISE012 = AT_WGS01 + 8 * KIB
+AT_TAB1 = AT_NOISE012 + 12 * KIB - EDGE
+AT_NOISE3 = AT_TAB1 + EDGE
 AT_NOISE4 = AT_NOISE3 + 4 * KIB
-AT_NOISE012 = AT_NOISE4 + 4 * KIB
-AT_WGS23 = AT_NOISE012 + 12 * KIB
-AT_TAB1 = AT_WGS23 + 8 * KIB - EDGE
-AT_NOISE5 = AT_TAB1 + EDGE
-AT_NOISE6 = AT_NOISE5 + 4 * KIB
+AT_NOISE5 = AT_NOISE4 + 4 * KIB
+AT_W4_SC_RAW = AT_NOISE5 + 4 * KIB
+AT_WGS23 = AT_W4_SC_RAW + 512
+AT_NOISE6 = AT_WGS23 + 8 * KIB
 AT_NOISE_LAST = AT_NOISE6 + 4 * KIB
-AT_W4_SC_RAW = AT_NOISE_LAST + 4 * KIB
-AT_PAGE1 = AT_W4_SC_RAW + 512
-AT_PAGE2 = AT_PAGE1 + 8 * KIB
-AT_W1_W0 = AT_PAGE2
-AT_HZ0 = AT_PAGE2 + 8 * KIB
+AT_W4_RAW = AT_NOISE_LAST + 4 * KIB
+AT_PAGE1 = AT_W4_RAW + 4 * KIB
+AT_HZ0 = AT_PAGE1 + 8 * KIB
 AT_HZ45 = AT_HZ0 + 16 * KIB
 AT_H67 = AT_HZ45 + 8 * KIB
 AT_TANH = AT_H67 + 8 * KIB
@@ -72,7 +72,7 @@ def tile_list_packet_loss_concealer_kernel(
 
         tab_sc = alloc([P, T], U8, "tab_sc")
         w1_sc_raw = alloc([P, H], U8, "w1_sc_raw")
-        w1_raw = alloc([P, PASSES, 2 * H], U8, "w1_raw")
+        w1_raw = place([P, PASSES, 2 * H], U8, "w1_raw", AT_PAGE1)
         nc.sync.dma_start(idx[:], offs)
         nc.sync.dma_start(tab_sc[0:32, :].bitcast(I32), tab_scales.rearrange("a q t -> (a q) t").bitcast(I32))
         nc.sync.dma_start(w1_sc_raw[0:32, :].bitcast(I32), w1_scales.rearrange("a q c -> (a q) c").bitcast(I32))
@@ -80,7 +80,7 @@ def tile_list_packet_loss_concealer_kernel(
         nc.sync.dma_start(idx2[:], offs2)
         nc.sync.dma_start(idx3[:], offs3)
         wgs_rows = wgs.rearrange("(i t) j -> i (t j)", t=PACK)
-        wgs0 = alloc([P, S], F32, "wgs0")
+        wgs_first = alloc([P, FIRST], F32, "wgs_first")
 
         def load_wgs(tile, first, start, stop, quadrants=range(4)):
             for q in quadrants:
@@ -88,7 +88,7 @@ def tile_list_packet_loss_concealer_kernel(
 
         tab_w = []
         for a in range(PASSES):
-            load_wgs(wgs0, 0, 0, S, (range(0, 1), range(1, 4))[a])
+            load_wgs(wgs_first, 0, 0, FIRST, (range(0, 1), range(1, 4))[a])
             t_w = place([P, T], I32, "tab_w%d" % a, (AT_TAB0, AT_TAB1)[a])
             nc.sync.dma_start(t_w[:], tab_words[a].rearrange("p t i -> p (t i)").bitcast(I32))
             tab_w.append(t_w)
@@ -98,7 +98,7 @@ def tile_list_packet_loss_concealer_kernel(
         planes = alloc([P, PASSES, S + H], U8, "planes")
         nc.vector.memset(planes[:, 1, :].bitcast(I32), 0)
         pages = [alloc([P, T2], F32, "page0"), None, None]
-        nc.vector.memset(pages[0][:], 0.0)
+        nc.gpsimd.memset(pages[0][:], 0.0)
 
         picked_sc = alloc([P, S], U8, "picked_sc")
         nc.vector.tensor_copy(picked_sc[:], tab_sc[:].indirect(idx[:]))
@@ -114,7 +114,7 @@ def tile_list_packet_loss_concealer_kernel(
         w1_w = {}
 
         def deal_w1(b):
-            w1_w[b] = place([P, PASSES, H], U8, "w1_w0", AT_W1_W0) if b == 0 else alloc([P, PASSES, H], U8, "w1_w1")
+            w1_w[b] = alloc([P, PASSES, H], U8, "w1_w%d" % b)
             nc.vector.tensor_copy(
                 w1_w[b][:].bitcast(U16).rearrange("p a (t c i) -> p a c t i", t=PACK, i=8),
                 w1_raw[:, :, b * H : (b + 1) * H].bitcast(U16).rearrange("p a (c i t) -> p a c t i", t=PACK, i=8),
@@ -123,26 +123,27 @@ def tile_list_packet_loss_concealer_kernel(
         deal_w1(0)
         deal_w1(1)
 
-        v_first = alloc([P, S], U32, "v_first")
+        v_first = place([P, S], U32, "v_first", AT_NOISE_LAST)
         nc.vector.tensor_copy(v_first[:], tab_w[0][:].bitcast(U32).indirect(idx[:]))
+        for i, at in ((1, AT_PAGE1), (2, AT_PAGE2)):
+            pages[i] = place([P, T2], F32, "page%d" % i, at)
+            nc.gpsimd.memset(pages[i][:], 0.0)
         v_w = {(0, half): v_first[:, half * HALF : (half + 1) * HALF] for half in range(2)}
         for half in range(2):
-            picked = alloc([P, HALF], U32, "v_second%d" % half)
+            picked = place([P, HALF], U32, "v_second%d" % half, (AT_NOISE6, AT_W4_RAW)[half])
             nc.vector.tensor_copy(picked[:], tab_w[1][:].bitcast(U32).indirect(idx[:, half * 32 : (half + 1) * 32]))
             v_w[1, half] = picked[:]
 
-        pages[1] = place([P, T2], F32, "page1", AT_PAGE1)
-        nc.gpsimd.memset(pages[1][:], 0.0)
 
-        wgs1 = place([P, S], F32, "wgs1", AT_WGS1)
+        wgs01 = place([P, 2 * S], F32, "wgs01", AT_WGS01)
         wgs23 = place([P, 2 * S], F32, "wgs23", AT_WGS23)
 
         def weights(s, cols):
             start, stop = (s % PACK) * S + cols.start, (s % PACK) * S + cols.stop
-            if stop <= S:
-                return wgs0[:, start:stop]
+            if stop <= FIRST:
+                return wgs_first[:, start:stop]
             if stop <= 2 * S:
-                return wgs1[:, start - S : stop - S]
+                return wgs01[:, start:stop]
             return wgs23[:, start - 2 * S : stop - 2 * S]
 
         noise_rows = noise.rearrange("(b p t) m -> p b t m", b=PASSES, t=PACK)
@@ -155,7 +156,8 @@ def tile_list_packet_loss_concealer_kernel(
             for i in range(count):
                 noise_of[first + i] = tile[:, i, :]
 
-        load_wgs(wgs1, S, S, 2 * S)
+        load_wgs(wgs01, 0, FIRST, S)
+        load_wgs(wgs01, 0, S, 2 * S)
         w3_raw = place([P, PASSES, PACK, N], F32, "w3_raw", AT_W3_RAW)
         w3_rows = w3.rearrange("(b p j) n -> b p j n", b=PASSES, j=PACK)
         for b in range(PASSES):
@@ -166,17 +168,10 @@ def tile_list_packet_loss_concealer_kernel(
         nc.sync.dma_start(gain_sb, gain.rearrange("(b p t) -> p b t", b=PASSES, t=PACK))
         load_noise(0, 3, AT_NOISE012)
         load_noise(3, 1, AT_NOISE3)
-        load_noise(4, 1, AT_NOISE4)
         load_wgs(wgs23, 2 * S, 2 * S, 4 * S)
+        load_noise(4, 1, AT_NOISE4)
         load_noise(5, 1, AT_NOISE5)
-        load_noise(6, 1, AT_NOISE6)
-        chunks = [slice(c0, c0 + CHUNK) for c0 in range(0, M, CHUNK)]
-        noise_last = {}
-        for cols in chunks:
-            noise_last[cols.start] = place([P, CHUNK], F32, "noise_last%d" % cols.start, AT_NOISE_LAST + 4 * cols.start)
-            nc.sync.dma_start(noise_last[cols.start][:], noise_rows[:, PASSES - 1, PACK - 1, cols])
-        w4_raw = alloc([P, PASSES, N], I32, "w4_raw", tag="w1_raw")
-        nc.sync.dma_start(w4_raw[:], w4_words.rearrange("a p c i -> p a (c i)").bitcast(I32))
+        load_wgs(wgs01, 0, 0, FIRST)
         w4_sc_raw = place([P, N], U8, "w4_sc_raw", AT_W4_SC_RAW)
         nc.vector.memset(w4_sc_raw[:].bitcast(I32), 0)
         for q in range(4):
@@ -218,8 +213,15 @@ def tile_list_packet_loss_concealer_kernel(
             for half in range(2):
                 project(s, slice(half * HALF, (half + 1) * HALF), HALF)
 
-        pages[2] = place([P, T2], F32, "page2", AT_PAGE2)
-        nc.gpsimd.memset(pages[2][:], 0.0)
+
+        load_noise(6, 1, AT_NOISE6)
+        chunks = [slice(c0, c0 + CHUNK) for c0 in range(0, M, CHUNK)]
+        noise_last = {}
+        for cols in chunks:
+            noise_last[cols.start] = place([P, CHUNK], F32, "noise_last%d" % cols.start, AT_NOISE_LAST + 4 * cols.start)
+            nc.sync.dma_start(noise_last[cols.start][:], noise_rows[:, PASSES - 1, PACK - 1, cols])
+        w4_raw = place([P, PASSES, N], I32, "w4_raw", AT_W4_RAW)
+        nc.sync.dma_start(w4_raw[:], w4_words.rearrange("a p c i -> p a (c i)").bitcast(I32))
 
         codes = {}
 

@@ -46,7 +46,7 @@ AT_HZ0 = AT_PAGE1 + 8 * KIB
 AT_HZ45 = AT_HZ0 + 16 * KIB
 AT_H67 = AT_HZ45 + 8 * KIB
 AT_TANH = AT_H67 + 8 * KIB
-AT_Y = AT_TANH - 512
+AT_Y = AT_TANH + 3 * KIB
 
 
 def tile_list_packet_loss_concealer_kernel(
@@ -370,10 +370,11 @@ def tile_list_packet_loss_concealer_kernel(
         def store_y(piece):
             width = piece.stop - piece.start
             per_bank = HALF // width
-            y_sb[piece.start] = place([P, PACK, width], F32, "y%d" % piece.start, (AT_Y if piece.start < HALF else AT_W3_RAW) + 16 * piece.start)
+            y_sb[piece.start] = place([P, PACK, width], F32, "y%d" % piece.start, AT_Y if piece.start == CHUNK else AT_W3_RAW + 16 * piece.start)
             for u in range(PACK // per_bank):
-                nc.scalar.copy(y_sb[piece.start][:, u * per_bank : (u + 1) * per_bank, :], y_banks[piece.start, u][:])
-            nc.sync.dma_start(y_rows[:, :, piece], y_sb[piece.start][:])
+                rows = slice(u * per_bank, (u + 1) * per_bank)
+                nc.scalar.copy(y_sb[piece.start][:, rows, :], y_banks[piece.start, u][:])
+                nc.sync.dma_start(y_rows[:, rows, piece], y_sb[piece.start][:, rows, :])
 
         def round_y(piece):
             nc.vector.tensor_copy(
@@ -387,15 +388,20 @@ def tile_list_packet_loss_concealer_kernel(
         gather(last, chunks[0])
         bend_plane(last, chunks[0:1])
         for k in range(len(chunks) + 1):
+            if k == 2:
+                store_y(pieces[0])
             if k + 1 < len(chunks):
                 gather(last, chunks[k + 1])
                 bend_plane(last, chunks[k + 1 : k + 2])
             if k >= 1:
                 finish(chunks[k - 1])
+            if k == 0:
+                first_d(chunks[0])
             if k < len(chunks):
-                first_d(chunks[k])
                 round_z(chunks[k])
-        for piece in pieces:
+            if k + 1 < len(chunks):
+                first_d(chunks[k + 1])
+        for piece in pieces[1:]:
             store_y(piece)
         round_y(pieces[0])
         for i, piece in enumerate(pieces):

@@ -26,23 +26,22 @@ CHUNK = 256
 KIB = 1024
 EDGE = 64
 
-AT_W3_RAW = 0
-AT_TAB0 = AT_W3_RAW + 16 * KIB - EDGE
+AT_NOISE012 = 0
+AT_TAB0 = AT_NOISE012 + 12 * KIB - EDGE
 AT_FACTORS = AT_TAB0 + EDGE
-AT_PAGE2 = AT_FACTORS + EDGE
-AT_WGS01 = AT_PAGE2 + 8 * KIB
-AT_NOISE012 = AT_WGS01 + 8 * KIB
-AT_TAB1 = AT_NOISE012 + 12 * KIB - EDGE
+AT_LATE_PLANES = AT_FACTORS + EDGE
+AT_WGS = AT_LATE_PLANES + 2 * KIB
+AT_W3_RAW = AT_WGS + 16 * KIB
+AT_TAB1 = AT_W3_RAW + 16 * KIB - EDGE
 AT_NOISE3 = AT_TAB1 + EDGE
 AT_NOISE4 = AT_NOISE3 + 4 * KIB
 AT_NOISE5 = AT_NOISE4 + 4 * KIB
-AT_W4_SC_RAW = AT_NOISE5 + 4 * KIB
-AT_WGS23 = AT_W4_SC_RAW + 512
-AT_NOISE6 = AT_WGS23 + 8 * KIB
+AT_NOISE6 = AT_TAB1 + 16 * KIB
 AT_NOISE_LAST = AT_NOISE6 + 4 * KIB
 AT_W4_RAW = AT_NOISE_LAST + 4 * KIB
 AT_PAGE1 = AT_W4_RAW + 4 * KIB
-AT_HZ0 = AT_PAGE1 + 8 * KIB
+AT_PAGE2 = AT_PAGE1 + 8 * KIB
+AT_HZ0 = AT_PAGE2 + 8 * KIB
 AT_HZ45 = AT_HZ0 + 16 * KIB
 AT_H67 = AT_HZ45 + 8 * KIB
 AT_TANH = AT_H67 + 8 * KIB
@@ -71,12 +70,13 @@ def tile_list_packet_loss_concealer_kernel(
         idx3 = lists.tile([P, M // 16], U16, name="idx3")
 
         tab_sc = alloc([P, T], U8, "tab_sc")
-        w1_sc_raw = alloc([P, H], U8, "w1_sc_raw")
+        sc_raw = place([P, H + N], U8, "sc_raw", AT_PAGE2)
         w1_raw = place([P, PASSES, 2 * H], U8, "w1_raw", AT_PAGE1)
+        nc.sync.dma_start(w1_raw[:].bitcast(I32), w1_words.rearrange("a p c -> p a c").bitcast(I32))
         nc.sync.dma_start(idx[:], offs)
         nc.sync.dma_start(tab_sc[0:32, :].bitcast(I32), tab_scales.rearrange("a q t -> (a q) t").bitcast(I32))
-        nc.sync.dma_start(w1_sc_raw[0:32, :].bitcast(I32), w1_scales.rearrange("a q c -> (a q) c").bitcast(I32))
-        nc.sync.dma_start(w1_raw[:].bitcast(I32), w1_words.rearrange("a p c -> p a c").bitcast(I32))
+        nc.sync.dma_start(sc_raw[0:32, 0:H].bitcast(I32), w1_scales.rearrange("a q c -> (a q) c").bitcast(I32))
+        nc.sync.dma_start(sc_raw[0:32, H : H + N].bitcast(I32), w4_scales.rearrange("a q c -> (a q) c").bitcast(I32))
         nc.sync.dma_start(idx2[:], offs2)
         nc.sync.dma_start(idx3[:], offs3)
         wgs_rows = wgs.rearrange("(i t) j -> i (t j)", t=PACK)
@@ -88,14 +88,15 @@ def tile_list_packet_loss_concealer_kernel(
 
         tab_w = []
         for a in range(PASSES):
-            load_wgs(wgs_first, 0, 0, FIRST, (range(0, 1), range(1, 4))[a])
+            if a == 1:
+                load_wgs(wgs_first, 0, 0, FIRST)
             t_w = place([P, T], I32, "tab_w%d" % a, (AT_TAB0, AT_TAB1)[a])
             nc.sync.dma_start(t_w[:], tab_words[a].rearrange("p t i -> p (t i)").bitcast(I32))
             tab_w.append(t_w)
-        for rows in (tab_sc, w1_sc_raw):
+        for rows in (tab_sc, sc_raw):
             nc.vector.memset(rows[32:64, :].bitcast(I32), 0)
             nc.vector.memset(rows[64:128, :].bitcast(I32), 0)
-        planes = alloc([P, PASSES, S + H], U8, "planes")
+        planes = alloc([P, PASSES, S + HALF], U8, "planes")
         nc.vector.memset(planes[:, 1, :].bitcast(I32), 0)
         pages = [alloc([P, T2], F32, "page0"), None, None]
         nc.gpsimd.memset(pages[0][:], 0.0)
@@ -103,13 +104,17 @@ def tile_list_packet_loss_concealer_kernel(
         picked_sc = alloc([P, S], U8, "picked_sc")
         nc.vector.tensor_copy(picked_sc[:], tab_sc[:].indirect(idx[:]))
         nc.vector.tensor_copy(
-            planes[:, 0, S : S + H].rearrange("p (b t c i) -> p b c t i", b=PASSES, t=PACK, i=16),
-            w1_sc_raw[:].rearrange("p (b c i t) -> p b c t i", b=PASSES, t=PACK, i=16),
+            planes[:, 0, S : S + HALF].rearrange("p (t c i) -> p c t i", t=PACK, i=16),
+            sc_raw[:, 0:HALF].rearrange("p (c i t) -> p c t i", t=PACK, i=16),
         )
         nc.vector.tensor_copy(planes[:, 0, 0:S].bitcast(I32), picked_sc[:].bitcast(I32))
-        for a, q in [divmod(n_move, 4) for n_move in range(1, PASSES * 4)]:
-            row = 16 * a + 4 * q
-            nc.sync.dma_start(planes[32 * q : 32 * q + 4, a, :].bitcast(I32), planes[row : row + 4, 0, :].bitcast(I32))
+
+        def move_rows(tile):
+            for a, q in [divmod(n_move, 4) for n_move in range(1, PASSES * 4)]:
+                row = 16 * a + 4 * q
+                nc.sync.dma_start(tile[32 * q : 32 * q + 4, a, :].bitcast(I32), tile[row : row + 4, 0, :].bitcast(I32))
+
+        move_rows(planes)
 
         w1_w = {}
 
@@ -125,6 +130,12 @@ def tile_list_packet_loss_concealer_kernel(
 
         v_first = place([P, S], U32, "v_first", AT_NOISE_LAST)
         nc.vector.tensor_copy(v_first[:], tab_w[0][:].bitcast(U32).indirect(idx[:]))
+        late_planes = place([P, PASSES, HALF + N], U8, "late_planes", AT_LATE_PLANES)
+        nc.vector.tensor_copy(
+            late_planes[:, 0, :].rearrange("p (b t c i) -> p b c t i", b=2, t=PACK, i=16),
+            sc_raw[:, HALF : H + N].rearrange("p (b c i t) -> p b c t i", b=2, t=PACK, i=16),
+        )
+        nc.vector.memset(late_planes[:, 1, :].bitcast(I32), 0)
         for i, at in ((1, AT_PAGE1), (2, AT_PAGE2)):
             pages[i] = place([P, T2], F32, "page%d" % i, at)
             nc.gpsimd.memset(pages[i][:], 0.0)
@@ -135,47 +146,40 @@ def tile_list_packet_loss_concealer_kernel(
             v_w[1, half] = picked[:]
 
 
-        wgs01 = place([P, 2 * S], F32, "wgs01", AT_WGS01)
-        wgs23 = place([P, 2 * S], F32, "wgs23", AT_WGS23)
+        wgs_sb = place([P, PACK * S], F32, "wgs_sb", AT_WGS)
 
         def weights(s, cols):
             start, stop = (s % PACK) * S + cols.start, (s % PACK) * S + cols.stop
-            if stop <= FIRST:
-                return wgs_first[:, start:stop]
-            if stop <= 2 * S:
-                return wgs01[:, start:stop]
-            return wgs23[:, start - 2 * S : stop - 2 * S]
+            return wgs_first[:, start:stop] if stop <= FIRST else wgs_sb[:, start:stop]
 
         noise_rows = noise.rearrange("(b p t) m -> p b t m", b=PASSES, t=PACK)
         noise_of = {}
 
-        def load_noise(first, count, at):
-            b, t = divmod(first, PACK)
-            tile = place([P, count, M], F32, "noise%d" % first, at)
-            nc.sync.dma_start(tile[:], noise_rows[:, b, t : t + count, :])
-            for i in range(count):
-                noise_of[first + i] = tile[:, i, :]
+        noise012 = place([P, 3, M], F32, "noise012", AT_NOISE012)
 
-        load_wgs(wgs01, 0, FIRST, S)
-        load_wgs(wgs01, 0, S, 2 * S)
-        w3_raw = place([P, PASSES, PACK, N], F32, "w3_raw", AT_W3_RAW)
-        w3_rows = w3.rearrange("(b p j) n -> b p j n", b=PASSES, j=PACK)
-        for b in range(PASSES):
-            nc.sync.dma_start(w3_raw[:, b], w3_rows[b])
+        def load_noise(s, at=None):
+            noise_of[s] = noise012[:, s, :] if at is None else place([P, M], F32, "noise%d" % s, at)[:]
+            nc.sync.dma_start(noise_of[s], noise_rows[:, s // PACK, s % PACK, :])
+
+        load_wgs(wgs_sb, 0, FIRST, S)
+        load_wgs(wgs_sb, 0, S, 2 * S)
+        move_rows(late_planes)
+        load_noise(0)
         factors = place([P, 2, PASSES, PACK], F32, "factors", AT_FACTORS)
         bend_sb, gain_sb = factors[:, 0], factors[:, 1]
         nc.sync.dma_start(bend_sb, bend.rearrange("(b p t) -> p b t", b=PASSES, t=PACK))
         nc.sync.dma_start(gain_sb, gain.rearrange("(b p t) -> p b t", b=PASSES, t=PACK))
-        load_noise(0, 3, AT_NOISE012)
-        load_noise(3, 1, AT_NOISE3)
-        load_wgs(wgs23, 2 * S, 2 * S, 4 * S)
-        load_noise(4, 1, AT_NOISE4)
-        load_noise(5, 1, AT_NOISE5)
-        load_wgs(wgs01, 0, 0, FIRST)
-        w4_sc_raw = place([P, N], U8, "w4_sc_raw", AT_W4_SC_RAW)
-        nc.vector.memset(w4_sc_raw[:].bitcast(I32), 0)
-        for q in range(4):
-            nc.sync.dma_start(w4_sc_raw[32 * q : 32 * q + 8, :].bitcast(I32), w4_scales[:, 4 * q : 4 * q + 4, :].bitcast(I32))
+        load_noise(1)
+        load_wgs(wgs_sb, 0, 2 * S, 4 * S)
+        load_noise(2)
+        load_wgs(wgs_sb, 0, 0, FIRST)
+        w3_raw = place([P, PASSES, PACK, N], F32, "w3_raw", AT_W3_RAW)
+        w3_rows = w3.rearrange("(b p j) n -> b p j n", b=PASSES, j=PACK)
+        for b in range(PASSES):
+            nc.sync.dma_start(w3_raw[:, b], w3_rows[b])
+        load_noise(3, AT_NOISE3)
+        load_noise(4, AT_NOISE4)
+        load_noise(5, AT_NOISE5)
 
         hz0 = place([P, PACK, S], F32, "hz0", AT_HZ0)
         hz45 = place([P, 2, S], F32, "hz45", AT_HZ45)
@@ -198,7 +202,7 @@ def tile_list_packet_loss_concealer_kernel(
                     nc.tensor.matmul_mx(
                         out=bank[:, c0 : c0 + width],
                         lhsT=w1_w[b][:, a, 2 * P * t : 2 * P * (t + 1)].bitcast(FP4X4),
-                        lhsT_scale=planes[:, a, S + P * s : S + P * (s + 1)],
+                        lhsT_scale=planes[:, a, S + P * t : S + P * (t + 1)] if b == 0 else late_planes[:, a, P * t : P * (t + 1)],
                         rhs=v_w[a, half][:, first + c0 : first + c0 + width].bitcast(FP8X4),
                         rhs_scale=planes[:, a, cols.start + c0 : cols.start + c0 + width],
                         start=(a == 1),
@@ -214,7 +218,7 @@ def tile_list_packet_loss_concealer_kernel(
                 project(s, slice(half * HALF, (half + 1) * HALF), HALF)
 
 
-        load_noise(6, 1, AT_NOISE6)
+        load_noise(6, AT_NOISE6)
         chunks = [slice(c0, c0 + CHUNK) for c0 in range(0, M, CHUNK)]
         noise_last = {}
         for cols in chunks:
@@ -247,17 +251,12 @@ def tile_list_packet_loss_concealer_kernel(
 
         def deal_w4():
             w4_w = place([P, PASSES, N], I32, "w4_w", AT_NOISE5)
-            w4_sc = alloc([P, N], U8, "w4_sc", tag="w1_sc_raw")
             nc.vector.tensor_copy(
                 w4_w[:].rearrange("p a (t c i) -> p a c t i", t=PACK, i=4),
                 w4_raw[:].rearrange("p a (c i t) -> p a c t i", t=PACK, i=4),
             )
-            nc.vector.tensor_copy(
-                w4_sc[:].rearrange("p (t c i) -> p c t i", t=PACK, i=16),
-                w4_sc_raw[:].rearrange("p (c i t) -> p c t i", t=PACK, i=16),
-            )
             for b in range(PASSES):
-                codes["w4", b] = (w4_w[:, b, :], w4_sc[4 * b : P, :])
+                codes["w4", b] = (w4_w[:, b, :], late_planes[:, b, HALF : HALF + N])
 
         def page_of(s):
             return pages[min(s, SLICES - 2) % 3]

@@ -342,13 +342,15 @@ def tile_list_packet_loss_concealer_kernel(
         d_sc0 = alloc([P, M], U8, "d_sc0")
 
         def first_d(cols):
-            words = place([P, CHUNK], U32, "d_w0_%d" % cols.start, AT_NOISE_LAST + 4 * cols.start)
+            at = AT_NOISE6 if cols.start == 0 else AT_NOISE_LAST + 4 * (cols.start - CHUNK)
+            words = place([P, CHUNK], U32, "d_w0_%d" % cols.start, at)
             nc.vector.quantize_mx(
                 out=words[:].bitcast(FP8X4), scales=d_sc0[:, cols], in_=d_bf[0][:, cols, :].rearrange("p m t -> p (m t)")
             )
             codes["d", 0] = (words, d_sc0)
             multiply("w4", "d", 0, cols, cols.start)
 
+        first_d(chunks[0])
         y_rows = out_0.rearrange("(p t) m -> p t m", t=PACK)
         y_words = alloc([P, M], I32, "y_words")
         y_scales = alloc([P, M], U8, "y_scales")
@@ -394,8 +396,6 @@ def tile_list_packet_loss_concealer_kernel(
                 bend_plane(last, chunks[k + 1 : k + 2])
             if k >= 1:
                 finish(chunks[k - 1])
-            if k == 0:
-                first_d(chunks[0])
             if k < len(chunks):
                 round_z(chunks[k])
             if k + 1 < len(chunks):

@@ -72,9 +72,9 @@ def tile_list_packet_loss_concealer_kernel(
         tab_sc = alloc([P, T], U8, "tab_sc")
         sc_raw = place([P, H + N], U8, "sc_raw", AT_PAGE2)
         w1_raw = place([P, PASSES, 2 * H], U8, "w1_raw", AT_PAGE1)
-        nc.sync.dma_start(w1_raw[:].bitcast(I32), w1_words.rearrange("a p c -> p a c").bitcast(I32))
         nc.sync.dma_start(idx[:], offs)
         nc.sync.dma_start(tab_sc[0:32, :].bitcast(I32), tab_scales.rearrange("a q t -> (a q) t").bitcast(I32))
+        nc.sync.dma_start(w1_raw[:].bitcast(I32), w1_words.rearrange("a p c -> p a c").bitcast(I32))
         nc.sync.dma_start(sc_raw[0:32, 0:H].bitcast(I32), w1_scales.rearrange("a q c -> (a q) c").bitcast(I32))
         nc.sync.dma_start(sc_raw[0:32, H : H + N].bitcast(I32), w4_scales.rearrange("a q c -> (a q) c").bitcast(I32))
         nc.sync.dma_start(idx2[:], offs2)
@@ -93,9 +93,9 @@ def tile_list_packet_loss_concealer_kernel(
             t_w = place([P, T], I32, "tab_w%d" % a, (AT_TAB0, AT_TAB1)[a])
             nc.sync.dma_start(t_w[:], tab_words[a].rearrange("p t i -> p (t i)").bitcast(I32))
             tab_w.append(t_w)
-        for rows in (tab_sc, sc_raw):
-            nc.vector.memset(rows[32:64, :].bitcast(I32), 0)
-            nc.vector.memset(rows[64:128, :].bitcast(I32), 0)
+        for rows, engine in ((tab_sc, nc.gpsimd), (sc_raw, nc.vector)):
+            engine.memset(rows[32:64, :].bitcast(I32), 0)
+            engine.memset(rows[64:128, :].bitcast(I32), 0)
         planes = alloc([P, PASSES, S + HALF], U8, "planes")
         nc.vector.memset(planes[:, 1, :].bitcast(I32), 0)
         pages = [alloc([P, T2], F32, "page0"), None, None]

@@ -26,17 +26,18 @@ CHUNK = 256
 KIB = 1024
 EDGE = 64
 
-AT_NOISE012 = 0
-AT_TAB0 = AT_NOISE012 + 12 * KIB - EDGE
-AT_FACTORS = AT_TAB0 + EDGE
+AT_TAB0 = 0
+AT_FACTORS = AT_TAB0
 AT_LATE_PLANES = AT_FACTORS + EDGE
-AT_WGS = AT_LATE_PLANES + 2 * KIB
-AT_W3_RAW = AT_WGS + 16 * KIB
+AT_W1_LATE = AT_LATE_PLANES + 2 * KIB
+AT_WGS01 = AT_W1_LATE + 2 * KIB
+AT_NOISE0 = AT_WGS01 + 8 * KIB
+AT_W3_RAW = AT_NOISE0 + 4 * KIB
 AT_TAB1 = AT_W3_RAW + 16 * KIB - EDGE
-AT_NOISE3 = AT_TAB1 + EDGE
-AT_NOISE4 = AT_NOISE3 + 4 * KIB
-AT_NOISE5 = AT_NOISE4 + 4 * KIB
-AT_NOISE6 = AT_TAB1 + 16 * KIB
+AT_WGS23 = AT_TAB1 + EDGE
+AT_NOISE1 = AT_WGS23 + 8 * KIB
+AT_NOISE2345 = AT_NOISE1 + 4 * KIB
+AT_NOISE6 = AT_NOISE2345 + 16 * KIB
 AT_NOISE_LAST = AT_NOISE6 + 4 * KIB
 AT_W4_RAW = AT_NOISE_LAST + 4 * KIB
 AT_PAGE1 = AT_W4_RAW + 4 * KIB
@@ -44,8 +45,7 @@ AT_PAGE2 = AT_PAGE1 + 8 * KIB
 AT_HZ0 = AT_PAGE2 + 8 * KIB
 AT_HZ45 = AT_HZ0 + 16 * KIB
 AT_H67 = AT_HZ45 + 8 * KIB
-AT_TANH = AT_H67 + 8 * KIB
-AT_Y = AT_TANH + 3 * KIB
+AT_Z_BF1 = AT_H67 + 8 * KIB
 
 
 def tile_list_packet_loss_concealer_kernel(
@@ -71,14 +71,13 @@ def tile_list_packet_loss_concealer_kernel(
 
         tab_sc = alloc([P, T], U8, "tab_sc")
         sc_raw = place([P, H + N], U8, "sc_raw", AT_PAGE2)
-        w1_raw = place([P, PASSES, 2 * H], U8, "w1_raw", AT_PAGE1)
+        w1_rows = w1_words.rearrange("a p c -> p a c").bitcast(I32)
+        w1_raw = [place([P, PASSES, H], U8, "w1_raw%d" % b, (AT_PAGE1, AT_W1_LATE)[b]) for b in range(PASSES)]
         nc.sync.dma_start(idx[:], offs)
         nc.sync.dma_start(tab_sc[0:32, :].bitcast(I32), tab_scales.rearrange("a q t -> (a q) t").bitcast(I32))
-        nc.sync.dma_start(w1_raw[:].bitcast(I32), w1_words.rearrange("a p c -> p a c").bitcast(I32))
+        nc.sync.dma_start(w1_raw[0][:].bitcast(I32), w1_rows[:, :, 0 : H // 4])
         nc.sync.dma_start(sc_raw[0:32, 0:H].bitcast(I32), w1_scales.rearrange("a q c -> (a q) c").bitcast(I32))
         nc.sync.dma_start(sc_raw[0:32, H : H + N].bitcast(I32), w4_scales.rearrange("a q c -> (a q) c").bitcast(I32))
-        nc.sync.dma_start(idx2[:], offs2)
-        nc.sync.dma_start(idx3[:], offs3)
         wgs_rows = wgs.rearrange("(i t) j -> i (t j)", t=PACK)
         wgs_first = alloc([P, FIRST], F32, "wgs_first")
 
@@ -89,6 +88,8 @@ def tile_list_packet_loss_concealer_kernel(
         tab_w = []
         for a in range(PASSES):
             if a == 1:
+                nc.sync.dma_start(idx2[:], offs2)
+                nc.sync.dma_start(idx3[:], offs3)
                 load_wgs(wgs_first, 0, 0, FIRST)
             t_w = place([P, T], I32, "tab_w%d" % a, (AT_TAB0, AT_TAB1)[a])
             nc.sync.dma_start(t_w[:], tab_words[a].rearrange("p t i -> p (t i)").bitcast(I32))
@@ -109,24 +110,23 @@ def tile_list_packet_loss_concealer_kernel(
         )
         nc.vector.tensor_copy(planes[:, 0, 0:S].bitcast(I32), picked_sc[:].bitcast(I32))
 
-        def move_rows(tile):
+        def move_rows(tile, queue):
             for a, q in [divmod(n_move, 4) for n_move in range(1, PASSES * 4)]:
                 row = 16 * a + 4 * q
-                nc.sync.dma_start(tile[32 * q : 32 * q + 4, a, :].bitcast(I32), tile[row : row + 4, 0, :].bitcast(I32))
+                queue.dma_start(tile[32 * q : 32 * q + 4, a, :].bitcast(I32), tile[row : row + 4, 0, :].bitcast(I32))
 
-        move_rows(planes)
+        move_rows(planes, nc.sync)
 
         w1_w = {}
 
-        def deal_w1(b):
+        def deal_w1(b, copy):
             w1_w[b] = alloc([P, PASSES, H], U8, "w1_w%d" % b)
-            nc.vector.tensor_copy(
+            copy(
                 w1_w[b][:].bitcast(U16).rearrange("p a (t c i) -> p a c t i", t=PACK, i=8),
-                w1_raw[:, :, b * H : (b + 1) * H].bitcast(U16).rearrange("p a (c i t) -> p a c t i", t=PACK, i=8),
+                w1_raw[b][:].bitcast(U16).rearrange("p a (c i t) -> p a c t i", t=PACK, i=8),
             )
 
-        deal_w1(0)
-        deal_w1(1)
+        deal_w1(0, nc.vector.tensor_copy)
 
         v_first = place([P, S], U32, "v_first", AT_NOISE_LAST)
         nc.vector.tensor_copy(v_first[:], tab_w[0][:].bitcast(U32).indirect(idx[:]))
@@ -142,50 +142,50 @@ def tile_list_packet_loss_concealer_kernel(
         v_w = {(0, half): v_first[:, half * HALF : (half + 1) * HALF] for half in range(2)}
         for half in range(2):
             picked = place([P, HALF], U32, "v_second%d" % half, (AT_NOISE6, AT_W4_RAW)[half])
-            nc.vector.tensor_copy(picked[:], tab_w[1][:].bitcast(U32).indirect(idx[:, half * 32 : (half + 1) * 32]))
+            for c0, c1 in ((0, FIRST), (FIRST, HALF)) if half == 0 else ((0, HALF),):
+                entries = idx[:, (half * HALF + c0) // 16 : (half * HALF + c1) // 16]
+                nc.vector.tensor_copy(picked[:, c0:c1], tab_w[1][:].bitcast(U32).indirect(entries))
             v_w[1, half] = picked[:]
 
 
-        wgs_sb = place([P, PACK * S], F32, "wgs_sb", AT_WGS)
+        wgs_sb = [place([P, 2 * S], F32, "wgs_sb%d" % u, at) for u, at in enumerate((AT_WGS01, AT_WGS23))]
 
         def weights(s, cols):
-            start, stop = (s % PACK) * S + cols.start, (s % PACK) * S + cols.stop
-            return wgs_first[:, start:stop] if stop <= FIRST else wgs_sb[:, start:stop]
+            u, e = divmod(s % PACK, 2)
+            return wgs_first[:, cols] if s % PACK == 0 and cols.stop <= FIRST else wgs_sb[u][:, e * S + cols.start : e * S + cols.stop]
 
         noise_rows = noise.rearrange("(b p t) m -> p b t m", b=PASSES, t=PACK)
         noise_of = {}
-
-        noise012 = place([P, 3, M], F32, "noise012", AT_NOISE012)
+        noise2345 = place([P, 4, M], F32, "noise2345", AT_NOISE2345)
 
         def load_noise(s, at=None):
-            noise_of[s] = noise012[:, s, :] if at is None else place([P, M], F32, "noise%d" % s, at)[:]
+            noise_of[s] = noise2345[:, s - 2, :] if at is None else place([P, M], F32, "noise%d" % s, at)[:]
             nc.sync.dma_start(noise_of[s], noise_rows[:, s // PACK, s % PACK, :])
 
-        load_wgs(wgs_sb, 0, FIRST, S)
-        load_wgs(wgs_sb, 0, S, 2 * S)
-        move_rows(late_planes)
-        load_noise(0)
+        load_wgs(wgs_sb[0], 0, FIRST, S)
+        nc.sync.dma_start(w1_raw[1][:].bitcast(I32), w1_rows[:, :, H // 4 : H // 2])
+        load_wgs(wgs_sb[0], 0, S, 2 * S)
+        move_rows(late_planes, nc.sync)
+        load_noise(0, AT_NOISE0)
         factors = place([P, 2, PASSES, PACK], F32, "factors", AT_FACTORS)
         bend_sb, gain_sb = factors[:, 0], factors[:, 1]
         nc.sync.dma_start(bend_sb, bend.rearrange("(b p t) -> p b t", b=PASSES, t=PACK))
         nc.sync.dma_start(gain_sb, gain.rearrange("(b p t) -> p b t", b=PASSES, t=PACK))
-        load_noise(1)
-        load_wgs(wgs_sb, 0, 2 * S, 4 * S)
-        load_noise(2)
-        load_wgs(wgs_sb, 0, 0, FIRST)
+        load_wgs(wgs_sb[0], 0, 0, FIRST)
         w3_raw = place([P, PASSES, PACK, N], F32, "w3_raw", AT_W3_RAW)
         w3_rows = w3.rearrange("(b p j) n -> b p j n", b=PASSES, j=PACK)
         for b in range(PASSES):
             nc.sync.dma_start(w3_raw[:, b], w3_rows[b])
-        load_noise(3, AT_NOISE3)
-        load_noise(4, AT_NOISE4)
-        load_noise(5, AT_NOISE5)
+        load_wgs(wgs_sb[1], 2 * S, 2 * S, 3 * S)
+        load_noise(1, AT_NOISE1)
+        load_wgs(wgs_sb[1], 2 * S, 3 * S, 4 * S)
+        for s in range(2, 6):
+            load_noise(s)
 
-        hz0 = place([P, PACK, S], F32, "hz0", AT_HZ0)
-        hz45 = place([P, 2, S], F32, "hz45", AT_HZ45)
-        h67 = place([P, 2, S], F32, "h67", AT_H67)
-        h_of = [hz0[:, t, :] for t in range(PACK)] + [hz45[:, 0, :], hz45[:, 1, :], h67[:, 0, :], h67[:, 1, :]]
-        z_of = h_of[:6] + h_of[2:4]
+        hz = place([P, 6, S], F32, "hz", AT_HZ0)
+        h67 = [place([P, S], F32, "h%d" % (6 + e), AT_H67 + 4 * KIB * e) for e in range(2)]
+        h_of = [hz[:, t, :] for t in range(6)] + [h67[0][:], h67[1][:]]
+        z_of = h_of[:6] + h_of[3:5]
         bank_count = [0]
 
         def next_bank(shape, name):
@@ -210,10 +210,12 @@ def tile_list_packet_loss_concealer_kernel(
                     )
             nc.scalar.activation(h_of[s][:, cols], bank[:], ACT.Square)
 
-        project(0, slice(0, FIRST), P)
-        project(0, slice(FIRST, HALF), P)
+        project(0, slice(0, FIRST), FIRST)
+        project(0, slice(FIRST, HALF), FIRST)
         project(0, slice(HALF, S), HALF)
         for s in range(1, SLICES):
+            if s == 2:
+                deal_w1(1, nc.scalar.copy)
             for half in range(2):
                 project(s, slice(half * HALF, (half + 1) * HALF), HALF)
 
@@ -245,21 +247,21 @@ def tile_list_packet_loss_concealer_kernel(
             )
 
         def quantise_w3(b):
-            at = (AT_NOISE3, AT_NOISE4)[b]
+            at = (AT_PAGE1, AT_NOISE2345)[b]
             codes["w3", b] = (place([P, N], U32, "w3_w%d" % b, at), place([P, N], U8, "w3_sc%d" % b, at + 2 * KIB))
             quantise("w3", b, w3_bf[b], slice(0, N))
 
         def deal_w4():
-            w4_w = place([P, PASSES, N], I32, "w4_w", AT_NOISE5)
-            nc.vector.tensor_copy(
+            w4_w = alloc([P, PASSES, N], U32, "w4_w")
+            nc.scalar.copy(
                 w4_w[:].rearrange("p a (t c i) -> p a c t i", t=PACK, i=4),
-                w4_raw[:].rearrange("p a (c i t) -> p a c t i", t=PACK, i=4),
+                w4_raw[:].bitcast(U32).rearrange("p a (c i t) -> p a c t i", t=PACK, i=4),
             )
             for b in range(PASSES):
                 codes["w4", b] = (w4_w[:, b, :], late_planes[:, b, HALF : HALF + N])
 
         def page_of(s):
-            return pages[min(s, SLICES - 2) % 3]
+            return pages[min(s, SLICES - 3) % 3]
 
         def scatter(s, cols):
             nc.vector.tensor_tensor(
@@ -274,20 +276,21 @@ def tile_list_packet_loss_concealer_kernel(
                 noise_of[s][:, cols] if s < SLICES - 1 else noise_last[cols.start][:], ALU.add,
             )
 
-        z_bf = [alloc([P, M, PACK], BF16, "z_bf%d" % b) for b in range(PASSES)]
+        tanh_early = place([P, M], F32, "tanh_early", AT_Z_BF1)
+        z_bf = [alloc([P, M, PACK], BF16, "z_bf0"), place([P, M, PACK], BF16, "z_bf1", AT_Z_BF1)]
         d_bf = [alloc([P, M, PACK], BF16, "d_bf%d" % b) for b in range(PASSES)]
 
-        tanh_sb = place([P, M], F32, "tanh_sb", AT_TANH)
+        tanh_sb = place([P, M], F32, "tanh_sb", AT_W3_RAW + 4 * KIB)
 
         def bend_plane(s, pieces_of_m):
             b, t = divmod(s, PACK)
-            tanh = z_of[s + 1] if s == SLICES - 2 else tanh_sb[:]
+            tanh = tanh_early[:] if s < SLICES - 2 else z_of[s + 1] if s == SLICES - 2 else tanh_sb[:]
             for cols in pieces_of_m:
                 nc.scalar.activation(tanh[:, cols], z_of[s][:, cols], ACT.Tanh, scale=bend_sb[:, b, t : t + 1])
             for cols in pieces_of_m:
                 nc.scalar.activation(d_bf[b][:, cols, t], tanh[:, cols], ACT.Copy, scale=gain_sb[:, b, t : t + 1])
 
-        for name, b in (("z", 0), ("z", 1), ("d", 1)):
+        for name, b in (("z", 1), ("d", 1)):
             codes[name, b] = (alloc([P, M], U32, "%s_w%d" % (name, b)), alloc([P, M], U8, "%s_sc%d" % (name, b)))
 
         pieces = [slice(0, 256), slice(256, 512), slice(512, 768), slice(768, 896), slice(896, 1024)]
@@ -321,20 +324,21 @@ def tile_list_packet_loss_concealer_kernel(
         scatter(0, slice(0, FIRST))
         scatter(0, slice(FIRST, S))
         for s in range(last):
-            if s + 1 < PACK:
+            if s + 1 < last - 1:
                 scatter(s + 1, everything)
-            if s >= PACK:
+            if s == last - 1:
+                quantise_w3(0)
                 scatter(s, everything)
-                if s - PACK < PASSES:
-                    quantise_w3(s - PACK)
-                else:
-                    deal_w4()
+                quantise_w3(1)
             gather(s, everything)
             bend_plane(s, [slice(0, HALF), slice(HALF, M)])
             if s % 2 == 1:
                 b, u = divmod(s // 2, 2)
-                pair = hz0[:, 2 * u : 2 * u + 2, :] if b == 0 else hz45[:]
+                pair = hz[:, s - 1 : s + 1, :]
                 nc.scalar.copy(z_bf[b][:, :, 2 * u : 2 * u + 2], pair.rearrange("p e m -> p m e"))
+            if s == 2:
+                deal_w4()
+        codes["z", 0] = (place([P, M], U32, "z_w0", AT_H67), alloc([P, M], U8, "z_sc0"))
         quantise("z", 0, z_bf[0], everything)
         multiply("w3", "z", 0, everything)
         scatter(last, everything)
@@ -355,7 +359,7 @@ def tile_list_packet_loss_concealer_kernel(
         y_words = alloc([P, M], I32, "y_words")
         y_scales = alloc([P, M], U8, "y_scales")
         codes["y", 0] = (y_words, y_scales)
-        y_bf = place([P, M, PACK], BF16, "y_bf", AT_NOISE012)
+        y_bf = place([P, M, PACK], BF16, "y_bf", AT_NOISE2345 + 8 * KIB)
         out_words = out_1[0].rearrange("p m t -> p (m t)").bitcast(I32)
         y_sb = {}
 
@@ -371,7 +375,7 @@ def tile_list_packet_loss_concealer_kernel(
         def store_y(piece):
             width = piece.stop - piece.start
             per_bank = HALF // width
-            y_sb[piece.start] = place([P, PACK, width], F32, "y%d" % piece.start, AT_Y if piece.start == CHUNK else AT_W3_RAW + 16 * piece.start)
+            y_sb[piece.start] = place([P, PACK, width], F32, "y%d" % piece.start, AT_W3_RAW + 16 * piece.start)
             for u in range(PACK // per_bank):
                 rows = slice(u * per_bank, (u + 1) * per_bank)
                 nc.scalar.copy(y_sb[piece.start][:, rows, :], y_banks[piece.start, u][:])
@@ -384,7 +388,7 @@ def tile_list_packet_loss_concealer_kernel(
             )
 
         def round_z(cols):
-            nc.vector.tensor_copy(z_bf[1][:, cols, 2:4], hz0[:, 2:4, cols].rearrange("p e m -> p m e"))
+            nc.vector.tensor_copy(z_bf[1][:, cols, 2:4], hz[:, 3:5, cols].rearrange("p e m -> p m e"))
 
         gather(last, chunks[0])
         bend_plane(last, chunks[0:1])

@@ -162,9 +162,10 @@ def tile_list_packet_loss_concealer_kernel(
             noise_of[s] = noise2345[:, s - 2, :] if at is None else place([P, M], F32, "noise%d" % s, at)[:]
             nc.sync.dma_start(noise_of[s], noise_rows[:, s // PACK, s % PACK, :])
 
+        load_wgs(wgs_sb[0], 0, S, S + FIRST)
         load_wgs(wgs_sb[0], 0, FIRST, S)
         nc.sync.dma_start(w1_raw[1][:].bitcast(I32), w1_rows[:, :, H // 4 : H // 2])
-        load_wgs(wgs_sb[0], 0, S, 2 * S)
+        load_wgs(wgs_sb[0], 0, S + FIRST, 2 * S)
         move_rows(late_planes, nc.sync)
         load_noise(0, AT_NOISE0)
         factors = place([P, 2, PASSES, PACK], F32, "factors", AT_FACTORS)
@@ -211,9 +212,11 @@ def tile_list_packet_loss_concealer_kernel(
             nc.scalar.activation(h_of[s][:, cols], bank[:], ACT.Square)
 
         project(0, slice(0, FIRST), FIRST)
-        project(0, slice(FIRST, HALF), FIRST)
-        project(0, slice(HALF, S), HALF)
-        for s in range(1, SLICES):
+        project(1, slice(0, FIRST), FIRST)
+        for s in range(2):
+            project(s, slice(FIRST, HALF), FIRST)
+            project(s, slice(HALF, S), HALF)
+        for s in range(2, SLICES):
             if s == 2:
                 deal_w1(1, nc.scalar.copy)
             for half in range(2):
@@ -321,10 +324,11 @@ def tile_list_packet_loss_concealer_kernel(
 
         everything = slice(0, M)
         last = SLICES - 1
-        scatter(0, slice(0, FIRST))
-        scatter(0, slice(FIRST, S))
+        for cols in (slice(0, FIRST), slice(FIRST, S)):
+            scatter(0, cols)
+            scatter(1, cols)
         for s in range(last):
-            if s + 1 < last - 1:
+            if 1 < s + 1 < last - 1:
                 scatter(s + 1, everything)
             if s == last - 1:
                 quantise_w3(0)

@@ -417,7 +417,6 @@ def tile_list_packet_loss_concealer_kernel(
             quantise("y", 0, y_bf, piece)
             if i == 2:
                 nc.sync.dma_start(out_words[:, 0 : piece.stop], y_words[:, 0 : piece.stop])
-        nc.scalar.dma_start(out_words[:, pieces[2].stop : M], y_words[:, pieces[2].stop : M])
+        nc.sync.dma_start(out_words[:, pieces[2].stop : M], y_words[:, pieces[2].stop : M])
         for q in range(4):
-            queue = nc.sync if q % 2 == 0 else nc.scalar
-            queue.dma_start(out_2[0][4 * q : 4 * q + 4, :].bitcast(I32), y_scales[32 * q : 32 * q + 4, :].bitcast(I32))
+            nc.sync.dma_start(out_2[0][4 * q : 4 * q + 4, :].bitcast(I32), y_scales[32 * q : 32 * q + 4, :].bitcast(I32))

@@ -111,7 +111,7 @@ def tile_list_packet_loss_concealer_kernel(
         nc.vector.tensor_copy(planes[:, 0, 0:S].bitcast(I32), picked_sc[:].bitcast(I32))
 
         def move_rows(tile, queue):
-            for a, q in [divmod(n_move, 4) for n_move in range(1, PASSES * 4)]:
+            for a, q in [(a, q) for a in range(PASSES) for q in (0, 2, 1, 3)][1:]:
                 row = 16 * a + 4 * q
                 queue.dma_start(tile[32 * q : 32 * q + 4, a, :].bitcast(I32), tile[row : row + 4, 0, :].bitcast(I32))
 
@@ -194,25 +194,25 @@ def tile_list_packet_loss_concealer_kernel(
             bank_count.append(bank_count.pop() + 1)
             return bank
 
-        def project(s, cols, width):
+        def project(s, cols, width, order=(1, 0)):
             b, t = divmod(s, PACK)
             half, first = divmod(cols.start, HALF)
             bank = next_bank([P, cols.stop - cols.start], "hbank%d_%d" % (s, cols.start))
             for c0 in range(0, cols.stop - cols.start, width):
-                for a in (1, 0):
+                for a in order:
                     nc.tensor.matmul_mx(
                         out=bank[:, c0 : c0 + width],
                         lhsT=w1_w[b][:, a, 2 * P * t : 2 * P * (t + 1)].bitcast(FP4X4),
                         lhsT_scale=planes[:, a, S + P * t : S + P * (t + 1)] if b == 0 else late_planes[:, a, P * t : P * (t + 1)],
                         rhs=v_w[a, half][:, first + c0 : first + c0 + width].bitcast(FP8X4),
                         rhs_scale=planes[:, a, cols.start + c0 : cols.start + c0 + width],
-                        start=(a == 1),
-                        stop=(a == 0),
+                        start=(a == order[0]),
+                        stop=(a == order[-1]),
                     )
             nc.scalar.activation(h_of[s][:, cols], bank[:], ACT.Square)
 
-        project(0, slice(0, FIRST), FIRST)
-        project(1, slice(0, FIRST), FIRST)
+        project(0, slice(0, FIRST), FIRST, (0, 1))
+        project(1, slice(0, FIRST), FIRST, (0, 1))
         for s in range(2):
             project(s, slice(FIRST, HALF), FIRST)
             project(s, slice(HALF, S), HALF)

from contextlib import ExitStack

import concourse.mybir as mybir

F32 = mybir.dt.float32
BF16 = mybir.dt.bfloat16
I32 = mybir.dt.int32
U32 = mybir.dt.uint32
U16 = mybir.dt.uint16
U8 = mybir.dt.uint8
FP8X4 = mybir.dt.float8_e4m3fn_x4
FP4X4 = mybir.dt.float4_e2m1fn_x4
ACT = mybir.ActivationFunctionType
ALU = mybir.AluOpType

K, H, N, T, S, T2, M = 1024, 1024, 512, 4096, 1024, 2048, 1024
FLOPS = 2 * K * H * S + 2 * 2 * H * N * M

P = 128
PACK = 4
PASSES = 2
SLICES = PASSES * PACK
HALF = 512
FIRST = 256
CHUNK = 256
KIB = 1024
EDGE = 64

AT_TAB0 = 0
AT_FACTORS = AT_TAB0
AT_LATE_PLANES = AT_FACTORS + EDGE
AT_W1_LATE = AT_LATE_PLANES + 2 * KIB
AT_WGS01 = AT_W1_LATE + 2 * KIB
AT_NOISE0 = AT_WGS01 + 8 * KIB
AT_W3_RAW = AT_NOISE0 + 4 * KIB
AT_TAB1 = AT_W3_RAW + 16 * KIB - EDGE
AT_WGS23 = AT_TAB1 + EDGE
AT_NOISE1 = AT_WGS23 + 8 * KIB
AT_NOISE2345 = AT_NOISE1 + 4 * KIB
AT_NOISE6 = AT_NOISE2345 + 16 * KIB
AT_NOISE_LAST = AT_NOISE6 + 4 * KIB
AT_W4_RAW = AT_NOISE_LAST + 4 * KIB
AT_PAGE1 = AT_W4_RAW + 4 * KIB
AT_PAGE2 = AT_PAGE1 + 8 * KIB
AT_HZ0 = AT_PAGE2 + 8 * KIB
AT_HZ45 = AT_HZ0 + 16 * KIB
AT_H67 = AT_HZ45 + 8 * KIB
AT_Z_BF1 = AT_H67 + 8 * KIB


def tile_list_packet_loss_concealer_kernel(
    tc, tab_words, tab_scales, offs, w1_words, w1_scales, wgs, offs2, offs3,
    noise, bend, gain, w3, w4_words, w4_scales, out_0, out_1, out_2,
):
    nc = tc.nc
    with ExitStack() as ctx:
        lists = ctx.enter_context(tc.tile_pool(name="lists", bufs=1))
        sb = ctx.enter_context(tc.tile_pool(name="sb", bufs=1))
        placed = ctx.enter_context(tc.tile_pool(name="placed", bufs=1))
        psum = ctx.enter_context(tc.psum_pool(name="psum", bufs=1))

        def alloc(shape, dtype, name, tag=None):
            return sb.tile(shape, dtype, name=name, tag=tag or name, align_bytes=64)

        def place(shape, dtype, name, at):
            return placed.tile(shape, dtype, name=name, tag=name, align_bytes=64, offset=at)

        idx = lists.tile([P, S // 16], U16, name="idx")
        idx2 = lists.tile([P, S // 16], U16, name="idx2")
        idx3 = lists.tile([P, M // 16], U16, name="idx3")

        tab_sc = alloc([P, T], U8, "tab_sc")
        sc_raw = place([P, H + N], U8, "sc_raw", AT_PAGE2)
        w1_rows = w1_words.rearrange("a p c -> p a c").bitcast(I32)
        w1_raw = [place([P, PASSES, H], U8, "w1_raw%d" % b, (AT_PAGE1, AT_W1_LATE)[b]) for b in range(PASSES)]
        nc.sync.dma_start(idx[:], offs)
        nc.sync.dma_start(tab_sc[0:32, :].bitcast(I32), tab_scales.rearrange("a q t -> (a q) t").bitcast(I32))
        nc.sync.dma_start(w1_raw[0][:].bitcast(I32), w1_rows[:, :, 0 : H // 4])
        nc.sync.dma_start(sc_raw[0:32, 0:H].bitcast(I32), w1_scales.rearrange("a q c -> (a q) c").bitcast(I32))
        nc.sync.dma_start(sc_raw[0:32, H : H + N].bitcast(I32), w4_scales.rearrange("a q c -> (a q) c").bitcast(I32))
        wgs_rows = wgs.rearrange("(i t) j -> i (t j)", t=PACK)
        wgs_first = alloc([P, FIRST], F32, "wgs_first")

        def load_wgs(tile, first, start, stop, quadrants=range(4)):
            for q in quadrants:
                nc.sync.dma_start(tile[32 * q : 32 * q + 32, start - first : stop - first], wgs_rows[:, start:stop])

        tab_w = []
        for a in range(PASSES):
            if a == 1:
                nc.sync.dma_start(idx2[:], offs2)
                nc.sync.dma_start(idx3[:], offs3)
                load_wgs(wgs_first, 0, 0, FIRST)
            t_w = place([P, T], I32, "tab_w%d" % a, (AT_TAB0, AT_TAB1)[a])
            nc.sync.dma_start(t_w[:], tab_words[a].rearrange("p t i -> p (t i)").bitcast(I32))
            tab_w.append(t_w)
        for rows, engine in ((tab_sc, nc.gpsimd), (sc_raw, nc.vector)):
            engine.memset(rows[32:64, :].bitcast(I32), 0)
            engine.memset(rows[64:128, :].bitcast(I32), 0)
        planes = alloc([P, PASSES, S + HALF], U8, "planes")
        nc.vector.memset(planes[:, 1, :].bitcast(I32), 0)
        pages = [alloc([P, T2], F32, "page0"), None, None]
        nc.gpsimd.memset(pages[0][:], 0.0)

        picked_sc = alloc([P, S], U8, "picked_sc")
        nc.vector.tensor_copy(picked_sc[:], tab_sc[:].indirect(idx[:]))
        nc.vector.tensor_copy(
            planes[:, 0, S : S + HALF].rearrange("p (t c i) -> p c t i", t=PACK, i=16),
            sc_raw[:, 0:HALF].rearrange("p (c i t) -> p c t i", t=PACK, i=16),
        )
        nc.vector.tensor_copy(planes[:, 0, 0:S].bitcast(I32), picked_sc[:].bitcast(I32))

        def move_rows(tile, queue):
            for a, q in [(a, q) for a in range(PASSES) for q in (0, 2, 1, 3)][1:]:
                row = 16 * a + 4 * q
                queue.dma_start(tile[32 * q : 32 * q + 4, a, :].bitcast(I32), tile[row : row + 4, 0, :].bitcast(I32))

        move_rows(planes, nc.sync)

        w1_w = {}

        def deal_w1(b, copy):
            w1_w[b] = alloc([P, PASSES, H], U8, "w1_w%d" % b)
            copy(
                w1_w[b][:].bitcast(U16).rearrange("p a (t c i) -> p a c t i", t=PACK, i=8),
                w1_raw[b][:].bitcast(U16).rearrange("p a (c i t) -> p a c t i", t=PACK, i=8),
            )

        deal_w1(0, nc.vector.tensor_copy)

        v_first = place([P, S], U32, "v_first", AT_NOISE_LAST)
        nc.vector.tensor_copy(v_first[:], tab_w[0][:].bitcast(U32).indirect(idx[:]))
        late_planes = place([P, PASSES, HALF + N], U8, "late_planes", AT_LATE_PLANES)
        nc.vector.tensor_copy(
            late_planes[:, 0, :].rearrange("p (b t c i) -> p b c t i", b=2, t=PACK, i=16),
            sc_raw[:, HALF : H + N].rearrange("p (b c i t) -> p b c t i", b=2, t=PACK, i=16),
        )
        nc.vector.memset(late_planes[:, 1, :].bitcast(I32), 0)
        for i, at in ((1, AT_PAGE1), (2, AT_PAGE2)):
            pages[i] = place([P, T2], F32, "page%d" % i, at)
            nc.gpsimd.memset(pages[i][:], 0.0)
        v_w = {(0, half): v_first[:, half * HALF : (half + 1) * HALF] for half in range(2)}
        for half in range(2):
            picked = place([P, HALF], U32, "v_second%d" % half, (AT_NOISE6, AT_W4_RAW)[half])
            for c0, c1 in ((0, FIRST), (FIRST, HALF)) if half == 0 else ((0, HALF),):
                entries = idx[:, (half * HALF + c0) // 16 : (half * HALF + c1) // 16]
                nc.vector.tensor_copy(picked[:, c0:c1], tab_w[1][:].bitcast(U32).indirect(entries))
            v_w[1, half] = picked[:]


        wgs_sb = [place([P, 2 * S], F32, "wgs_sb%d" % u, at) for u, at in enumerate((AT_WGS01, AT_WGS23))]

        def weights(s, cols):
            u, e = divmod(s % PACK, 2)
            return wgs_first[:, cols] if s % PACK == 0 and cols.stop <= FIRST else wgs_sb[u][:, e * S + cols.start : e * S + cols.stop]

        noise_rows = noise.rearrange("(b p t) m -> p b t m", b=PASSES, t=PACK)
        noise_of = {}
        noise2345 = place([P, 4, M], F32, "noise2345", AT_NOISE2345)

        def load_noise(s, at=None):
            noise_of[s] = noise2345[:, s - 2, :] if at is None else place([P, M], F32, "noise%d" % s, at)[:]
            nc.sync.dma_start(noise_of[s], noise_rows[:, s // PACK, s % PACK, :])

        load_wgs(wgs_sb[0], 0, S, S + FIRST)
        load_wgs(wgs_sb[0], 0, FIRST, S)
        nc.sync.dma_start(w1_raw[1][:].bitcast(I32), w1_rows[:, :, H // 4 : H // 2])
        load_wgs(wgs_sb[0], 0, S + FIRST, 2 * S)
        move_rows(late_planes, nc.sync)
        load_noise(0, AT_NOISE0)
        factors = place([P, 2, PASSES, PACK], F32, "factors", AT_FACTORS)
        bend_sb, gain_sb = factors[:, 0], factors[:, 1]
        nc.sync.dma_start(bend_sb, bend.rearrange("(b p t) -> p b t", b=PASSES, t=PACK))
        nc.sync.dma_start(gain_sb, gain.rearrange("(b p t) -> p b t", b=PASSES, t=PACK))
        load_wgs(wgs_sb[0], 0, 0, FIRST)
        w3_raw = place([P, PASSES, PACK, N], F32, "w3_raw", AT_W3_RAW)
        w3_rows = w3.rearrange("(b p j) n -> b p j n", b=PASSES, j=PACK)
        for b in range(PASSES):
            nc.sync.dma_start(w3_raw[:, b], w3_rows[b])
        load_wgs(wgs_sb[1], 2 * S, 2 * S, 3 * S)
        load_noise(1, AT_NOISE1)
        load_wgs(wgs_sb[1], 2 * S, 3 * S, 4 * S)
        for s in range(2, 6):
            load_noise(s)

        hz = place([P, 6, S], F32, "hz", AT_HZ0)
        h67 = [place([P, S], F32, "h%d" % (6 + e), AT_H67 + 4 * KIB * e) for e in range(2)]
        h_of = [hz[:, t, :] for t in range(6)] + [h67[0][:], h67[1][:]]
        z_of = h_of[:6] + h_of[3:5]
        bank_count = [0]

        def next_bank(shape, name):
            bank = psum.tile(shape, F32, name=name, tag="bank%d" % (bank_count[0] % 8))
            bank_count.append(bank_count.pop() + 1)
            return bank

        def project(s, cols, width, order=(1, 0)):
            b, t = divmod(s, PACK)
            half, first = divmod(cols.start, HALF)
            bank = next_bank([P, cols.stop - cols.start], "hbank%d_%d" % (s, cols.start))
            for c0 in range(0, cols.stop - cols.start, width):
                for a in order:
                    nc.tensor.matmul_mx(
                        out=bank[:, c0 : c0 + width],
                        lhsT=w1_w[b][:, a, 2 * P * t : 2 * P * (t + 1)].bitcast(FP4X4),
                        lhsT_scale=planes[:, a, S + P * t : S + P * (t + 1)] if b == 0 else late_planes[:, a, P * t : P * (t + 1)],
                        rhs=v_w[a, half][:, first + c0 : first + c0 + width].bitcast(FP8X4),
                        rhs_scale=planes[:, a, cols.start + c0 : cols.start + c0 + width],
                        start=(a == order[0]),
                        stop=(a == order[-1]),
                    )
            nc.scalar.activation(h_of[s][:, cols], bank[:], ACT.Square)

        project(0, slice(0, FIRST), FIRST, (0, 1))
        project(1, slice(0, FIRST), FIRST, (0, 1))
        for s in range(2):
            project(s, slice(FIRST, HALF), FIRST)
            project(s, slice(HALF, S), HALF)
        for s in range(2, SLICES):
            if s == 2:
                deal_w1(1, nc.scalar.copy)
            for half in range(2):
                project(s, slice(half * HALF, (half + 1) * HALF), HALF)


        load_noise(6, AT_NOISE6)
        chunks = [slice(c0, c0 + CHUNK) for c0 in range(0, M, CHUNK)]
        noise_last = {}
        for cols in chunks:
            noise_last[cols.start] = place([P, CHUNK], F32, "noise_last%d" % cols.start, AT_NOISE_LAST + 4 * cols.start)
            nc.sync.dma_start(noise_last[cols.start][:], noise_rows[:, PASSES - 1, PACK - 1, cols])
        w4_raw = place([P, PASSES, N], I32, "w4_raw", AT_W4_RAW)
        nc.sync.dma_start(w4_raw[:], w4_words.rearrange("a p c i -> p a (c i)").bitcast(I32))

        codes = {}

        def quantise(name, b, source, cols):
            words, scales = codes[name, b]
            nc.vector.quantize_mx(
                out=words[:, cols].bitcast(FP8X4),
                scales=scales[:, cols],
                in_=source[:, cols, :].rearrange("p m t -> p (m t)"),
            )

        w3_bf = [alloc([P, N, PACK], BF16, "w3_bf%d" % b) for b in range(PASSES)]
        for b in range(PASSES):
            nc.scalar.copy(
                w3_bf[b][:].rearrange("p (t m) j -> p m t j", t=PACK),
                w3_raw[:, b].rearrange("p j (m t) -> p m t j", t=PACK),
            )

        def quantise_w3(b):
            at = (AT_PAGE1, AT_NOISE2345)[b]
            codes["w3", b] = (place([P, N], U32, "w3_w%d" % b, at), place([P, N], U8, "w3_sc%d" % b, at + 2 * KIB))
            quantise("w3", b, w3_bf[b], slice(0, N))

        def deal_w4():
            w4_w = alloc([P, PASSES, N], U32, "w4_w")
            nc.scalar.copy(
                w4_w[:].rearrange("p a (t c i) -> p a c t i", t=PACK, i=4),
                w4_raw[:].bitcast(U32).rearrange("p a (c i t) -> p a c t i", t=PACK, i=4),
            )
            for b in range(PASSES):
                codes["w4", b] = (w4_w[:, b, :], late_planes[:, b, HALF : HALF + N])

        def page_of(s):
            return pages[min(s, SLICES - 3) % 3]

        def scatter(s, cols):
            nc.vector.tensor_tensor(
                page_of(s)[:].indirect(idx2[:, cols.start // 16 : cols.stop // 16]),
                h_of[s][:, cols], weights(s, cols), ALU.mult,
            )

        def gather(s, cols):
            nc.vector.tensor_tensor(
                z_of[s][:, cols],
                page_of(s)[:].indirect(idx3[:, cols.start // 16 : cols.stop // 16]),
                noise_of[s][:, cols] if s < SLICES - 1 else noise_last[cols.start][:], ALU.add,
            )

        tanh_early = place([P, M], F32, "tanh_early", AT_Z_BF1)
        z_bf = [alloc([P, M, PACK], BF16, "z_bf0"), place([P, M, PACK], BF16, "z_bf1", AT_Z_BF1)]
        d_bf = [alloc([P, M, PACK], BF16, "d_bf%d" % b) for b in range(PASSES)]

        tanh_sb = place([P, M], F32, "tanh_sb", AT_W3_RAW + 4 * KIB)

        def bend_plane(s, pieces_of_m):
            b, t = divmod(s, PACK)
            tanh = tanh_early[:] if s < SLICES - 2 else z_of[s + 1] if s == SLICES - 2 else tanh_sb[:]
            for cols in pieces_of_m:
                nc.scalar.activation(tanh[:, cols], z_of[s][:, cols], ACT.Tanh, scale=bend_sb[:, b, t : t + 1])
            for cols in pieces_of_m:
                nc.scalar.activation(d_bf[b][:, cols, t], tanh[:, cols], ACT.Copy, scale=gain_sb[:, b, t : t + 1])

        for name, b in (("z", 1), ("d", 1)):
            codes[name, b] = (alloc([P, M], U32, "%s_w%d" % (name, b)), alloc([P, M], U8, "%s_sc%d" % (name, b)))

        pieces = [slice(0, 256), slice(256, 512), slice(512, 768), slice(768, 896), slice(896, 1024)]
        y_banks = {}

        def multiply(weight, moving, b, cols, words_from=0):
            opens = b == 0 and moving == "z"
            closes = b == PASSES - 1 and moving == "z"
            for piece in pieces:
                if piece.start < cols.start or piece.stop > cols.stop:
                    continue
                width = piece.stop - piece.start
                per_bank = HALF // width
                for t in range(PACK):
                    u, e = divmod(t, per_bank)
                    if opens and e == 0:
                        y_banks[piece.start, u] = next_bank([P, per_bank, width], "ybank%d_%d" % (piece.start, u))
                    n_cols = slice(t * P, (t + 1) * P)
                    nc.tensor.matmul_mx(
                        out=y_banks[piece.start, u][:, e, :],
                        lhsT=codes[weight, b][0][:, n_cols].bitcast(FP8X4),
                        lhsT_scale=codes[weight, b][1][:, n_cols],
                        rhs=codes[moving, b][0][:, piece.start - words_from : piece.stop - words_from].bitcast(FP8X4),
                        rhs_scale=codes[moving, b][1][:, piece],
                        start=(opens and e == 0),
                        stop=(closes and e == per_bank - 1),
                    )

        everything = slice(0, M)
        last = SLICES - 1
        for cols in (slice(0, FIRST), slice(FIRST, S)):
            scatter(0, cols)
            scatter(1, cols)
        for s in range(last):
            if 1 < s + 1 < last - 1:
                scatter(s + 1, everything)
            if s == last - 1:
                quantise_w3(0)
                scatter(s, everything)
                quantise_w3(1)
            gather(s, everything)
            bend_plane(s, [slice(0, HALF), slice(HALF, M)])
            if s % 2 == 1:
                b, u = divmod(s // 2, 2)
                pair = hz[:, s - 1 : s + 1, :]
                nc.scalar.copy(z_bf[b][:, :, 2 * u : 2 * u + 2], pair.rearrange("p e m -> p m e"))
            if s == 2:
                deal_w4()
        codes["z", 0] = (place([P, M], U32, "z_w0", AT_H67), alloc([P, M], U8, "z_sc0"))
        quantise("z", 0, z_bf[0], everything)
        multiply("w3", "z", 0, everything)
        scatter(last, everything)

        d_sc0 = alloc([P, M], U8, "d_sc0")

        def first_d(cols):
            at = AT_NOISE6 if cols.start == 0 else AT_NOISE_LAST + 4 * (cols.start - CHUNK)
            words = place([P, CHUNK], U32, "d_w0_%d" % cols.start, at)
            nc.vector.quantize_mx(
                out=words[:].bitcast(FP8X4), scales=d_sc0[:, cols], in_=d_bf[0][:, cols, :].rearrange("p m t -> p (m t)")
            )
            codes["d", 0] = (words, d_sc0)
            multiply("w4", "d", 0, cols, cols.start)

        first_d(chunks[0])
        y_rows = out_0.rearrange("(p t) m -> p t m", t=PACK)
        y_words = alloc([P, M], I32, "y_words")
        y_scales = alloc([P, M], U8, "y_scales")
        codes["y", 0] = (y_words, y_scales)
        y_bf = place([P, M, PACK], BF16, "y_bf", AT_NOISE2345 + 8 * KIB)
        out_words = out_1[0].rearrange("p m t -> p (m t)").bitcast(I32)
        y_sb = {}

        def finish(cols):
            quantise("d", 1, d_bf[1], cols)
            quantise("z", 1, z_bf[1], cols)
            for piece in pieces:
                if piece.start < cols.start or piece.stop > cols.stop:
                    continue
                multiply("w4", "d", 1, piece)
                multiply("w3", "z", 1, piece)

        def store_y(piece):
            width = piece.stop - piece.start
            per_bank = HALF // width
            y_sb[piece.start] = place([P, PACK, width], F32, "y%d" % piece.start, AT_W3_RAW + 16 * piece.start)
            for u in range(PACK // per_bank):
                rows = slice(u * per_bank, (u + 1) * per_bank)
                nc.scalar.copy(y_sb[piece.start][:, rows, :], y_banks[piece.start, u][:])
                nc.sync.dma_start(y_rows[:, rows, piece], y_sb[piece.start][:, rows, :])

        def round_y(piece):
            nc.vector.tensor_copy(
                y_bf[:, piece, :].rearrange("p (c i) t -> p c t i", i=4),
                y_sb[piece.start][:].rearrange("p t (c i) -> p c t i", i=4),
            )

        def round_z(cols):
            nc.vector.tensor_copy(z_bf[1][:, cols, 2:4], hz[:, 3:5, cols].rearrange("p e m -> p m e"))

        gather(last, chunks[0])
        bend_plane(last, chunks[0:1])
        for k in range(len(chunks) + 1):
            if k == 2:
                store_y(pieces[0])
            if k + 1 < len(chunks):
                gather(last, chunks[k + 1])
                bend_plane(last, chunks[k + 1 : k + 2])
            if k >= 1:
                finish(chunks[k - 1])
            if k < len(chunks):
                round_z(chunks[k])
            if k + 1 < len(chunks):
                first_d(chunks[k + 1])
        for piece in pieces[1:]:
            store_y(piece)
        round_y(pieces[0])
        for i, piece in enumerate(pieces):
            if i + 1 < len(pieces):
                round_y(pieces[i + 1])
            quantise("y", 0, y_bf, piece)
            if i == 2:
                nc.sync.dma_start(out_words[:, 0 : piece.stop], y_words[:, 0 : piece.stop])
        nc.sync.dma_start(out_words[:, pieces[2].stop : M], y_words[:, pieces[2].stop : M])
        for q in range(4):
            nc.sync.dma_start(out_2[0][4 * q : 4 * q + 4, :].bitcast(I32), y_scales[32 * q : 32 * q + 4, :].bitcast(I32))
